import numpy as np
import ml_dtypes


def mxq(x, axis, fmt="e4m3"):
    dtype, down = {"e4m3": (ml_dtypes.float8_e4m3fn, 7), "e5m2": (ml_dtypes.float8_e5m2, 14)}[fmt]
    v = np.moveaxis(np.asarray(x, np.float32).astype(ml_dtypes.bfloat16).astype(np.float64), axis, -1)
    blocks = v.reshape(v.shape[:-1] + (-1, 32))
    amax = np.abs(blocks).max(-1, keepdims=True)
    byte = np.maximum(np.where(amax > 0, np.frexp(amax)[1] - 1 + 127, 0) - down, 1)
    scale = np.exp2(byte - 127.0)
    codes = (blocks / scale).astype(np.float32).astype(dtype).astype(np.float64)
    return np.moveaxis((codes * scale).reshape(v.shape), -1, axis)


WIDE = False


def mx_kscale(k):
    if not WIDE:
        return np.ones(k)
    levels = np.array([10, -10, 5, -5, 0])
    if k % 512:
        return np.exp2(np.random.permutation(np.resize(levels, k // 32))).repeat(32)
    a = np.empty((k // 512, 16))
    for p in range(k // 512):
        a[p, :8] = np.random.permutation(np.resize(levels, 8))
        for g in range(8):
            far = levels[np.abs(levels - a[p, g]) >= 10]
            a[p, g + 8] = far[np.random.randint(len(far))]
    return np.exp2(a.ravel()).repeat(32)


BF16 = ml_dtypes.bfloat16


def bf(x):
    return np.asarray(x, np.float32).astype(BF16)


def f64(x):
    return np.asarray(x).astype(np.float64)


E2M1 = np.array([0.0, 0.5, 1.0, 1.5, 2.0, 3.0, 4.0, 6.0, -0.0, -0.5, -1.0, -1.5, -2.0, -3.0, -4.0, -6.0])


def pack_weight(w, fmt):
    k, n = w.shape
    w = f64(bf(w)).reshape(k // 32, 32, n)
    amax = np.abs(w).max(1)
    if fmt == "e4m3":
        byte = np.frexp(amax)[1] - 1 + 127 - 7
    else:
        mant, ex = np.frexp(amax / 6.0)
        byte = np.where(mant > 0.5, ex, ex - 1) + 127
    byte = np.clip(np.where(amax > 0, byte, 1), 1, 254)
    scaled = (w * np.exp2(127.0 - byte)[:, None, :]).reshape(k, n).astype(np.float32)
    by_word = np.ascontiguousarray(scaled.reshape(k // 512, 128, 4, n).transpose(0, 1, 3, 2))
    if fmt == "e4m3":
        words = by_word.astype(ml_dtypes.float8_e4m3fn).view(np.uint8)
    else:
        c = by_word.astype(ml_dtypes.float4_e2m1fn).view(np.uint8) & 0xF
        words = c[..., 0::2] | (c[..., 1::2] << 4)
    return np.ascontiguousarray(words), np.ascontiguousarray(byte.astype(np.uint8).reshape(k // 512, 16, n))


def unpack_weight(words, scales, fmt):
    g, p, n, _ = words.shape
    if fmt == "e4m3":
        vals = np.ascontiguousarray(words).view(ml_dtypes.float8_e4m3fn).astype(np.float64)
    else:
        nib = np.empty((g, p, n, 4), np.uint8)
        nib[..., 0::2] = words & 0xF
        nib[..., 1::2] = words >> 4
        vals = E2M1[nib]
    vals = vals * np.repeat(np.exp2(scales.astype(np.float64) - 127.0), 8, axis=1)[..., None]
    return vals.transpose(0, 1, 3, 2).reshape(g * 512, n)
def pack4(w):
    words, scales = pack_weight(w, "e2m1")
    return words.reshape(words.shape[0], 128, -1), scales


def unpack4(words, scales):
    return unpack_weight(words.reshape(words.shape[0], 128, -1, 2), scales, "e2m1")


B, P, S, K, C = 2, 1024, 512, 1024, 512


def instance_norm(x):
    mu = np.mean(x, axis=1, keepdims=True)
    centered = x - mu
    var = np.mean(centered * centered, axis=1, keepdims=True)
    return centered / np.sqrt(var + 1e-5)


def draw0():
    s, t = mx_kscale(S), mx_kscale(K)
    x = bf(0.5 + 1.5 * np.random.standard_normal((B, P, C)))
    m = bf(np.random.standard_normal((B, P, S)) * s)
    wm_words, wm_scales = pack4(np.random.standard_normal((S, K)) / np.sqrt(S) / s[:, None])
    bm = bf(0.3 * np.random.standard_normal(K))
    g = bf(np.random.standard_normal(K) * t)
    wg_words, wg_scales = pack4(np.random.standard_normal((K, C)) / np.sqrt(K) / t[:, None])
    wb_words, wb_scales = pack4(np.random.standard_normal((K, C)) / np.sqrt(K) / t[:, None])
    return {
        "x": x,
        "m": m,
        "wm_words": wm_words,
        "wm_scales": wm_scales,
        "bm": bm,
        "g": g,
        "wg_words": wg_words,
        "wg_scales": wg_scales,
        "wb_words": wb_words,
        "wb_scales": wb_scales,
    }


def core(x, m, wm_words, wm_scales, bm, g, wg_words, wg_scales, wb_words, wb_scales):
    h = (mxq(f64(m), 2, "e4m3") @ unpack4(wm_words, wm_scales)) + f64(bm)[None, None, :]
    a = np.maximum(h, 0.0) * f64(g)[None, None, :]
    aq = mxq(a, 2, "e4m3")
    gamma = aq @ unpack4(wg_words, wg_scales)
    beta = aq @ unpack4(wb_words, wb_scales)
    xn = instance_norm(f64(x))
    y = xn * (1.0 + gamma) + beta
    return np.where(y >= 0.0, y, 0.2 * y)


def e4m3fn_bytes(y):
    return np.clip(np.asarray(y, np.float64), -448.0, 448.0).astype(np.float32).astype(ml_dtypes.float8_e4m3fn).view(np.uint8)


def e4m3fn_values(b):
    return np.asarray(b, np.uint8).view(ml_dtypes.float8_e4m3fn).astype(np.float64)


def setup_inputs():
    d = draw0()
    x0 = np.asarray(d['m']).astype(np.float64)
    s = (np.max(np.abs(x0), axis=(0, 1), keepdims=True) / 448.0).astype(np.float32)
    out = {}
    for k, v in d.items():
        if k == 'm':
            out['m_bytes'] = e4m3fn_bytes(x0 / s.astype(np.float64))
            out['m_scale'] = s
        else:
            out[k] = v
    return out


def reference(x, m_bytes, m_scale, wm_words, wm_scales, bm, g, wg_words, wg_scales, wb_words, wb_scales):
    return core(x, e4m3fn_values(m_bytes) * m_scale.astype(np.float64), wm_words, wm_scales, bm, g, wg_words, wg_scales, wb_words, wb_scales)

@@ -1,0 +1,319 @@
+from contextlib import ExitStack
+
+import concourse.mybir as mybir
+from concourse.masks import make_identity
+
+B, T, S, K, C = 2, 1024, 512, 1024, 512
+FLOPS = 2 * B * T * (S * K + 2 * K * C)
+
+P = 128
+TILES = T // P
+CHUNK = 4
+COLS = CHUNK * P
+CB = C // P
+
+F32 = mybir.dt.float32
+BF16 = mybir.dt.bfloat16
+I32 = mybir.dt.int32
+U32 = mybir.dt.uint32
+U8 = mybir.dt.uint8
+F8 = mybir.dt.float8_e4m3fn
+E4M3 = mybir.dt.float8_e4m3fn_x4
+E2M1 = mybir.dt.float4_e2m1fn_x4
+ALU = mybir.AluOpType
+ACT = mybir.ActivationFunctionType
+
+
+def tile_spademodulationpointwise_w4_kernel(
+    tc, x, m_bytes, m_scale, wm_words, wm_scales, bm, g, wg_words, wg_scales, wb_words, wb_scales, out
+):
+    nc = tc.nc
+    with ExitStack() as ctx:
+        keep = ctx.enter_context(tc.tile_pool(name="keep", bufs=1))
+        mpool = ctx.enter_context(tc.tile_pool(name="mpool", bufs=4))
+        apool = ctx.enter_context(tc.tile_pool(name="apool", bufs=4))
+        qpool = ctx.enter_context(tc.tile_pool(name="qpool", bufs=4))
+        xpool = ctx.enter_context(tc.tile_pool(name="xpool", bufs=6))
+        ypool = ctx.enter_context(tc.tile_pool(name="ypool", bufs=3))
+        ps_s = ctx.enter_context(tc.psum_pool(name="ps_s", bufs=5))
+        ps_gb = ctx.enter_context(tc.psum_pool(name="ps_gb", bufs=3))
+
+        ident_f = keep.tile([P, P], F32, name="ident_f")
+        ident_b = keep.tile([P, P], BF16, name="ident_b")
+        ones = keep.tile([P, 1], BF16, name="ones")
+        minus_half = keep.tile([P, 1], F32, name="minus_half")
+        wm_sc_raw = keep.tile([P, K], U8, name="wm_sc_raw")
+        wgb_sc = keep.tile([P, 4, C], U8, name="wgb_sc", align_bytes=64)
+        nc.vector.memset(wm_sc_raw[:].bitcast(I32), 0)
+        nc.vector.memset(wgb_sc[:].rearrange("p a n -> p (a n)").bitcast(I32), 0)
+        make_identity(nc, ident_f[:])
+        nc.gpsimd.tensor_copy(out=ident_b[:], in_=ident_f[:])
+        nc.gpsimd.memset(ones[:], 1.0)
+        nc.gpsimd.memset(minus_half[:], -0.5)
+
+        scale_bc = keep.tile([P, S], F32, name="scale_bc")
+        nc.scalar.dma_start(out=scale_bc[:], in_=m_scale.rearrange("a o k -> (a o k)").partition_broadcast(P))
+        m_u8 = []
+        for c in range(4):
+            mt = keep.tile([P, CHUNK, S], U8, name="m_u8_%d" % c)
+            m_u8.append(mt)
+
+        def load_m(c):
+            s, i0 = c // 2, (c % 2) * CHUNK
+            nc.sync.dma_start(out=m_u8[c][:], in_=m_bytes[s].rearrange("(p i) k -> p i k", i=TILES)[:, i0 : i0 + CHUNK, :])
+
+        x_sb = []
+        for s in range(B):
+            xt = keep.tile([P, TILES, C], BF16, name="x_sb_%d" % s)
+            x_sb.append(xt)
+
+        def load_x(s):
+            nc.sync.dma_start(out=x_sb[s][:], in_=x[s].rearrange("(p i) c -> p i c", i=TILES))
+
+        b_raw = keep.tile([P, 2, 4], BF16, name="b_raw")
+        g_raw = keep.tile([P, 2, 4], BF16, name="g_raw")
+        wm_raw = keep.tile([P, 2 * K], U8, name="wm_raw")
+        wgb = keep.tile([P, 4, 2 * C], U8, name="wgb", align_bytes=64)
+
+        load_m(0)
+        for q in range(4):
+            nc.sync.dma_start(out=wm_sc_raw[32 * q : 32 * q + 4, :].bitcast(I32), in_=wm_scales[0, 4 * q : 4 * q + 4, :].bitcast(I32))
+        nc.sync.dma_start(out=wm_raw[:], in_=wm_words[0])
+        nc.scalar.dma_start(out=b_raw[:], in_=bm.rearrange("(a p t) -> p a t", p=P, t=4))
+        nc.scalar.dma_start(out=g_raw[:], in_=g.rearrange("(a p t) -> p a t", p=P, t=4))
+        load_m(1)
+        load_x(0)
+        load_m(2)
+        load_m(3)
+        for w, scales in ((0, wg_scales), (2, wb_scales)):
+            for q in range(4):
+                nc.sync.dma_start(
+                    out=wgb_sc[32 * q : 32 * q + 4, w : w + 2, :].bitcast(I32),
+                    in_=scales[:, 4 * q : 4 * q + 4, :].rearrange("a q n -> q a n").bitcast(I32),
+                )
+        nc.sync.dma_start(out=wgb[:, 0:2, :], in_=wg_words.rearrange("a p n -> p a n"))
+        nc.sync.dma_start(out=wgb[:, 2:4, :], in_=wb_words.rearrange("a p n -> p a n"))
+        load_x(1)
+
+        sgn = keep.tile([P, 2, 4], F32, name="sgn")
+        gabs = keep.tile([P, 2, 4], F32, name="gabs")
+        gb = keep.tile([P, 2, 4], F32, name="gb")
+        nc.gpsimd.tensor_scalar(out=sgn[:], in0=g_raw[:], scalar1=0.0, scalar2=2.0, op0=ALU.is_ge, op1=ALU.mult)
+        nc.gpsimd.tensor_scalar(out=sgn[:], in0=sgn[:], scalar1=-1.0, scalar2=None, op0=ALU.add)
+        nc.gpsimd.tensor_tensor(out=gabs[:], in0=g_raw[:], in1=sgn[:], op=ALU.mult)
+        nc.gpsimd.tensor_tensor(out=gb[:], in0=b_raw[:], in1=gabs[:], op=ALU.mult)
+
+        wm_w = keep.tile([P, 2, 4, 2 * P], U8, name="wm_w", align_bytes=64)
+        wm_sc = keep.tile([P, 2, 4, P], U8, name="wm_sc", align_bytes=64)
+
+        def permute_wm(a):
+            nc.vector.tensor_copy(
+                out=wm_w[:, a].rearrange("p t (m b) -> p t m b", b=2),
+                in_=wm_raw[:].rearrange("p (a m t b) -> p a t m b", a=2, t=4, b=2)[:, a],
+            )
+            nc.vector.tensor_copy(
+                out=wm_sc[:, a], in_=wm_sc_raw[:].rearrange("p (a m t) -> p a t m", a=2, t=4)[:, a]
+            )
+
+        mq, mqs, mgrp, mbank = {}, {}, {}, {}
+
+        m_bf = {}
+
+        def widen(i):
+            c, j = divmod(i, CHUNK)
+            m_bf[i] = mpool.tile([P, S], BF16, tag="m_bf", name="m_bf_t", bufs=12)
+            nc.vector.tensor_tensor(out=m_bf[i][:], in0=m_u8[c][:, j, :].bitcast(F8), in1=scale_bc[:], op=ALU.mult)
+
+        mbank = {}
+
+        def turn_pe(c, h):
+            mbank[c, h] = ps_s.tile([P, 2, 2, P], F32, tag="s", name="mbank_t")
+            for j in range(2):
+                words = m_bf[CHUNK * c + 2 * h + j][:].bitcast(F32)
+                for u in range(2):
+                    nc.tensor.transpose(mbank[c, h][:, j, u, :], words[:, u : S // 2 : 2], ident_f[:])
+
+        def turn_out(c, h):
+            if h == 0:
+                mgrp[c] = mpool.tile([P, CHUNK, P, 4], BF16, tag="m_grouped", name="m_grouped", bufs=3, align_bytes=64)
+            nc.scalar.copy(
+                out=mgrp[c][:, 2 * h : 2 * h + 2].rearrange("p j r t -> p (j r t)").bitcast(F32).rearrange("p (j r u) -> p j r u", j=2, u=2),
+                in_=mbank[c, h][:].rearrange("p j u r -> p j r u"),
+            )
+
+        def quant_m(c):
+            mq[c] = qpool.tile([P, COLS], U32, tag="mq", name="mq_t", align_bytes=64)
+            mqs[c] = qpool.tile([P, COLS], U8, tag="mqs", name="mqs_t", align_bytes=64)
+            nc.vector.quantize_mx(out=mq[c][:].bitcast(E4M3), scales=mqs[c][:], in_=mgrp[c][:].rearrange("p j r t -> p (j r t)"))
+
+        aq, aqs, planes, grouped = {}, {}, {}, {}
+
+        hbank = {}
+
+        def embed_pe(k, t):
+            c, a = divmod(k, 2)
+            hbank[k, t] = ps_s.tile([P, COLS], F32, tag="s", name="hbank_t")
+            nc.tensor.matmul_mx(
+                out=hbank[k, t][:],
+                lhsT=wm_w[:, a, t, :].bitcast(E2M1),
+                lhsT_scale=wm_sc[:, a, t, :],
+                rhs=mq[c][:].bitcast(E4M3),
+                rhs_scale=mqs[c][:],
+                start=True,
+                stop=True,
+            )
+
+        def embed_out(k, t):
+            a = k % 2
+            if t == 0:
+                planes[k] = apool.tile([P, 4, COLS], BF16, tag="planes", name="planes")
+            nc.scalar.activation(
+                out=planes[k][:, t, :], in_=hbank[k, t][:], func=ACT.Relu, bias=gb[:, a, t : t + 1], scale=gabs[:, a, t : t + 1]
+            )
+
+        def apply_sign(k, t):
+            a = k % 2
+            nc.vector.tensor_scalar(
+                out=planes[k][:, t, :], in0=planes[k][:, t, :], scalar1=sgn[:, a, t : t + 1], scalar2=None, op0=ALU.mult
+            )
+
+        def interleave(k, copy):
+            grouped[k] = apool.tile([P, COLS, 4], BF16, tag="a_grouped", name="a_grouped", align_bytes=64)
+            copy(
+                out=grouped[k][:].rearrange("p (n i) t -> p n t i", i=4),
+                in_=planes[k][:].rearrange("p t (n i) -> p n t i", i=4),
+            )
+
+        def quant_a(k):
+            aq[k] = qpool.tile([P, COLS], U32, tag="aq", name="aq_t", align_bytes=64, bufs=6)
+            aqs[k] = qpool.tile([P, COLS], U8, tag="aqs", name="aqs_t", align_bytes=64, bufs=6)
+            nc.vector.quantize_mx(out=aq[k][:].bitcast(E4M3), scales=aqs[k][:], in_=grouped[k][:].rearrange("p n t -> p (n t)"))
+
+        neg_mu, xt_ps, xt, rstd = {}, {}, {}, {}
+
+        sums = {}
+
+        def mean_pe(s):
+            sums[s] = ps_s.tile([P, CB], F32, tag="s", name="sums_t")
+            for cb in range(CB):
+                for i in range(TILES):
+                    nc.tensor.matmul(
+                        out=sums[s][:, cb : cb + 1],
+                        lhsT=x_sb[s][:, i, cb * P : (cb + 1) * P],
+                        rhs=ones[:],
+                        start=(i == 0),
+                        stop=(i == TILES - 1),
+                    )
+
+        def mean_out(s):
+            neg_mu[s] = xpool.tile([P, CB], F32, tag="neg_mu", name="neg_mu")
+            nc.scalar.activation(out=neg_mu[s][:], in_=sums[s][:], func=ACT.Copy, scale=-1.0 / T)
+
+        def x_var(s, cb):
+            junk = xpool.tile([P, TILES, P], BF16, tag="junk", name="junk", bufs=1)
+            ss = xpool.tile([P, 1], F32, tag="ss", name="ss")
+            nc.scalar.activation(out=junk[:], in_=xt_ps[s, cb][:], func=ACT.Square, bias=neg_mu[s][:, cb : cb + 1], accum_out=ss[:])
+            rstd[s, cb] = xpool.tile([P, 1], F32, tag="rstd", name="rstd_t", bufs=8)
+            nc.gpsimd.tensor_scalar(out=ss[:], in0=ss[:], scalar1=1.0 / T, scalar2=1e-5, op0=ALU.mult, op1=ALU.add)
+            nc.gpsimd.tensor_tensor(out=rstd[s, cb][:], in0=ss[:], in1=minus_half[:], op=ALU.pow)
+
+        def center_pe(s, cb):
+            xt_ps[s, cb] = ps_s.tile([P, TILES, P], BF16, tag="s", name="xt_ps_t")
+            for i in range(TILES):
+                nc.tensor.transpose(xt_ps[s, cb][:, i, :], x_sb[s][:, i, cb * P : (cb + 1) * P], ident_b[:])
+
+        def x_center(s, cb):
+            xt[s, cb] = xpool.tile([P, TILES, P], F32, tag="xt", name="xt_t", bufs=8)
+            nc.scalar.activation(out=xt[s, cb][:], in_=xt_ps[s, cb][:], func=ACT.Identity, bias=neg_mu[s][:, cb : cb + 1])
+
+        gam, bet, t1s, ys, lks = {}, {}, {}, {}, {}
+
+        def project(u, w):
+            c, cb = divmod(u, CB)
+            bank = ps_gb.tile([P, COLS], F32, tag="gb", name="bank_gb")
+            (gam if w == 0 else bet)[u] = bank
+            for a in range(2):
+                nc.tensor.matmul_mx(
+                    out=bank[:],
+                    lhsT=wgb[:, w + a, 2 * P * cb : 2 * P * (cb + 1)].bitcast(E2M1),
+                    lhsT_scale=wgb_sc[:, w + a, P * cb : P * (cb + 1)],
+                    rhs=aq[2 * c + a][:].bitcast(E4M3),
+                    rhs_scale=aqs[2 * c + a][:],
+                    start=(a == 0),
+                    stop=(a == 1),
+                )
+
+        def modulate(u):
+            c, cb = divmod(u, CB)
+            s, i0 = c // 2, (c % 2) * CHUNK
+            t1s[u] = ypool.tile([P, COLS], F32, tag="t1", name="t1_t", bufs=6)
+            nc.vector.scalar_tensor_tensor(
+                out=t1s[u][:], in0=gam[u][:], scalar=1.0, in1=xt[s, cb][:, i0 : i0 + CHUNK, :].rearrange("p i r -> p (i r)"), op0=ALU.add, op1=ALU.mult
+            )
+
+        def shift(u):
+            c, cb = divmod(u, CB)
+            ys[u] = ypool.tile([P, COLS], F32, tag="y", name="y_t", bufs=6)
+            nc.vector.scalar_tensor_tensor(
+                out=ys[u][:], in0=t1s[u][:], scalar=rstd[c // 2, cb][:], in1=bet[u][:], op0=ALU.mult, op1=ALU.add
+            )
+
+        def leaky(u):
+            lks[u] = ypool.tile([P, CHUNK, P], F32, tag="lk", name="lk_t", bufs=6)
+            nc.vector.scalar_tensor_tensor(
+                out=lks[u][:].rearrange("p i r -> p (i r)"), in0=ys[u][:], scalar=0.2, in1=ys[u][:], op0=ALU.mult, op1=ALU.max
+            )
+
+        obank = {}
+
+        def out_pe(u):
+            obank[u] = ps_s.tile([P, CHUNK, P], F32, tag="s", name="obank_t")
+            for i in range(CHUNK):
+                nc.tensor.transpose(obank[u][:, i, :], lks[u][:, i, :], ident_f[:])
+
+        def out_store(u):
+            c, cb = divmod(u, CB)
+            s, i0 = c // 2, (c % 2) * CHUNK
+            res = ypool.tile([P, CHUNK, P], F32, tag="res", name="res_t", bufs=6)
+            nc.scalar.copy(out=res[:], in_=obank[u][:])
+            nc.sync.dma_start(
+                out=out[s].rearrange("(p i) c -> p i c", i=TILES)[:, i0 : i0 + CHUNK, cb * P : (cb + 1) * P], in_=res[:]
+            )
+
+        calls = {
+            "W": lambda c, j: widen(CHUNK * c + j),
+            "P": lambda z, a: permute_wm(a),
+            "T": turn_pe, "X": turn_out, "MQ": lambda c, z: quant_m(c),
+            "EP": embed_pe, "E": embed_out, "SG": apply_sign,
+            "CP": lambda k, z: interleave(k, nc.vector.tensor_copy), "AQ": lambda k, z: quant_a(k),
+            "MP": lambda s, z: mean_pe(s), "M": lambda s, z: mean_out(s),
+            "NP": center_pe, "N": x_center, "Q": x_var, "G": lambda s, b: None,
+            "GM": lambda c, b: project(CB * c + b, 0), "BT": lambda c, b: project(CB * c + b, 2),
+            "V1": lambda c, b: modulate(CB * c + b), "V2": lambda c, b: shift(CB * c + b), "V3": lambda c, b: leaky(CB * c + b),
+            "OP": lambda c, b: out_pe(CB * c + b), "O": lambda c, b: out_store(CB * c + b),
+        }
+        order = """
+            W.0.0 W.0.1 T.0.0 W.0.2 W.0.3 T.0.1 P.0.0 X.0.0 X.0.1 P.0.1 MQ.0.0 EP.0.0 EP.0.1 EP.0.2 EP.0.3 MP.0.0
+            E.0.0 E.0.1 E.0.2 E.0.3 W.1.0 W.1.1 T.1.0 W.1.2 W.1.3 T.1.1 W.3.0 W.3.1 SG.0.0 SG.0.1 SG.0.2 SG.0.3
+            CP.0.0 AQ.0.0 EP.1.0 EP.1.1 M.0.0 EP.1.2 X.1.0 EP.1.3 W.3.2 X.1.1 MQ.1.0 EP.3.0 E.1.0 EP.3.1 E.1.1 EP.3.2
+            E.1.2 EP.3.3 E.1.3 W.3.3 SG.1.0 SG.1.1 SG.1.2 SG.1.3 E.3.0 E.3.1 E.3.2 E.3.3 EP.2.0 EP.2.1 EP.2.2 EP.2.3
+            NP.0.0 E.2.0 MP.1.0 W.2.0 E.2.1 NP.0.1 E.2.2 E.2.3 N.0.0 CP.1.0 NP.0.2 W.2.1 AQ.1.0 GM.0.0 N.0.1 T.2.0
+            Q.0.0 NP.0.3 W.2.2 W.2.3 M.1.0 T.2.1 SG.3.0 SG.3.1 SG.3.2 SG.3.3 CP.3.0 GM.0.1 N.0.2 SG.2.0 SG.2.1 SG.2.2
+            SG.2.3 CP.2.0 AQ.2.0 GM.0.2 N.0.3 AQ.3.0 V1.0.0 GM.1.0 V1.0.1 GM.0.3 V1.0.2 BT.0.0 V1.1.0 GM.1.1 V1.0.3 BT.0.1
+            V2.0.0 GM.1.2 Q.0.1 X.2.0 X.2.1 MQ.2.0 EP.5.0 Q.0.2 EP.5.1 EP.5.2 Q.0.3 EP.5.3 V1.1.1 BT.0.2 T.3.0 V3.0.0
+            E.5.0 T.3.1 V2.0.1 BT.0.3 V1.1.2 BT.1.0 V2.0.2 GM.1.3 V3.0.1 SG.5.0 E.5.1 SG.5.1 E.5.2 SG.5.2 E.5.3 SG.5.3
+            EP.4.0 EP.4.1 EP.4.2 X.3.0 EP.4.3 V3.0.2 V2.0.3 BT.1.1 CP.5.0 X.3.1 MQ.3.0 EP.6.0 E.4.0 EP.6.1 E.4.1 EP.6.2
+            E.4.2 EP.6.3 SG.4.0 SG.4.1 SG.4.2 E.4.3 SG.4.3 CP.4.0 V3.0.3 NP.1.0 V2.1.0 BT.1.2 V1.1.3 BT.1.3 E.6.0 E.6.1
+            E.6.2 E.6.3 NP.1.1 AQ.4.0 AQ.5.0 V2.1.1 GM.2.0 N.1.0 OP.0.0 NP.1.2 OP.0.1 V3.1.0 V2.1.2 BT.2.0 Q.1.0 OP.0.2
+            V2.1.3 GM.2.1 N.1.1 Q.1.1 OP.0.3 V3.1.1 V1.2.0 BT.2.1 O.0.0 EP.7.0 N.1.2 Q.1.2 EP.7.1 O.0.1 EP.7.2 O.0.2
+            EP.7.3 O.0.3 NP.1.3 V3.1.2 SG.6.0 SG.6.1 SG.6.2 SG.6.3 CP.6.0 V2.2.0 GM.2.2 V1.2.1 BT.2.2 V3.1.3 E.7.0 OP.1.0
+            E.7.1 E.7.2 E.7.3 OP.1.1 V2.2.1 BT.2.3 V1.2.2 GM.2.3 OP.1.2 SG.7.0 SG.7.1 SG.7.2 SG.7.3 CP.7.0 N.1.3 OP.1.3
+            V1.2.3 V2.2.2 V3.2.0 Q.1.3 OP.2.0 O.1.0 V3.2.1 OP.2.1 V2.2.3 O.1.1 V3.2.2 OP.2.2 O.1.2 V3.2.3 OP.2.3 O.1.3
+            AQ.6.0 AQ.7.0 GM.3.0 V1.3.0 BT.3.0 V2.3.0 GM.3.1 V1.3.1 BT.3.1 V2.3.1 GM.3.2 V1.3.2 BT.3.2 V2.3.2 O.2.0 O.2.1
+            GM.3.3 V1.3.3 BT.3.3 V2.3.3 O.2.2 O.2.3 V3.3.0 V3.3.1 V3.3.2 V3.3.3 OP.3.0 OP.3.1 OP.3.2 OP.3.3 O.3.0 O.3.1
+            O.3.2 O.3.3
+        """
+        ctx.enter_context(tc.manual_schedule())
+        for word in order.split():
+            name, a, b = word.split(".")
+            calls[name](int(a), int(b))

@@ -45,14 +45,23 @@ def tile_spademodulationpointwise_w4_kernel(
         wm_sc_raw = keep.tile([P, K], U8, name="wm_sc_raw")
         wgb_sc = keep.tile([P, 4, C], U8, name="wgb_sc", align_bytes=64)
         nc.vector.memset(wm_sc_raw[:].bitcast(I32), 0)
-        nc.vector.memset(wgb_sc[:].rearrange("p a n -> p (a n)").bitcast(I32), 0)
         make_identity(nc, ident_f[:])
         nc.gpsimd.tensor_copy(out=ident_b[:], in_=ident_f[:])
         nc.gpsimd.memset(ones[:], 1.0)
+        nc.gpsimd.memset(wgb_sc[:].rearrange("p a n -> p (a n)").bitcast(I32), 0)
         nc.gpsimd.memset(minus_half[:], -0.5)
 
         scale_bc = keep.tile([P, S], F32, name="scale_bc")
-        nc.scalar.dma_start(out=scale_bc[:], in_=m_scale.rearrange("a o k -> (a o k)").partition_broadcast(P))
+        scale_col = keep.tile([P, 4], F32, name="scale_col")
+        nc.scalar.dma_start(out=scale_col[:], in_=m_scale.rearrange("a o (p j) -> p (a o j)", j=4))
+        b_raw = keep.tile([P, 2, 4], BF16, name="b_raw")
+        g_raw = keep.tile([P, 2, 4], BF16, name="g_raw")
+        nc.scalar.dma_start(out=b_raw[:], in_=bm.rearrange("(a p t) -> p a t", p=P, t=4))
+        nc.scalar.dma_start(out=g_raw[:], in_=g.rearrange("(a p t) -> p a t", p=P, t=4))
+        scale_ps = ps_s.tile([P, 4, P], F32, tag="s", name="scale_ps")
+        for j in range(4):
+            nc.tensor.transpose(scale_ps[:, j, :], scale_col[:, j : j + 1].to_broadcast([P, P]), ident_f[:])
+        nc.scalar.copy(out=scale_bc[:].rearrange("p (k j) -> p k j", j=4), in_=scale_ps[:].rearrange("p j k -> p k j"))
         m_u8 = []
         for c in range(4):
             mt = keep.tile([P, CHUNK, S], U8, name="m_u8_%d" % c)
@@ -70,21 +79,16 @@ def tile_spademodulationpointwise_w4_kernel(
         def load_x(s):
             nc.sync.dma_start(out=x_sb[s][:], in_=x[s].rearrange("(p i) c -> p i c", i=TILES))
 
-        b_raw = keep.tile([P, 2, 4], BF16, name="b_raw")
-        g_raw = keep.tile([P, 2, 4], BF16, name="g_raw")
         wm_raw = keep.tile([P, 2 * K], U8, name="wm_raw")
         wgb = keep.tile([P, 4, 2 * C], U8, name="wgb", align_bytes=64)
 
-        load_m(0)
         for q in range(4):
             nc.sync.dma_start(out=wm_sc_raw[32 * q : 32 * q + 4, :].bitcast(I32), in_=wm_scales[0, 4 * q : 4 * q + 4, :].bitcast(I32))
+        load_m(0)
         nc.sync.dma_start(out=wm_raw[:], in_=wm_words[0])
-        nc.scalar.dma_start(out=b_raw[:], in_=bm.rearrange("(a p t) -> p a t", p=P, t=4))
-        nc.scalar.dma_start(out=g_raw[:], in_=g.rearrange("(a p t) -> p a t", p=P, t=4))
         load_m(1)
         load_x(0)
         load_m(2)
-        load_m(3)
         for w, scales in ((0, wg_scales), (2, wb_scales)):
             for q in range(4):
                 nc.sync.dma_start(
@@ -93,6 +97,7 @@ def tile_spademodulationpointwise_w4_kernel(
                 )
         nc.sync.dma_start(out=wgb[:, 0:2, :], in_=wg_words.rearrange("a p n -> p a n"))
         nc.sync.dma_start(out=wgb[:, 2:4, :], in_=wb_words.rearrange("a p n -> p a n"))
+        load_m(3)
         load_x(1)
 
         sgn = keep.tile([P, 2, 4], F32, name="sgn")
@@ -293,24 +298,24 @@ def tile_spademodulationpointwise_w4_kernel(
             "OP": lambda c, b: out_pe(CB * c + b), "O": lambda c, b: out_store(CB * c + b),
         }
         order = """
-            W.0.0 W.0.1 T.0.0 W.0.2 W.0.3 T.0.1 P.0.0 X.0.0 X.0.1 P.0.1 MQ.0.0 EP.0.0 EP.0.1 EP.0.2 EP.0.3 MP.0.0
-            E.0.0 E.0.1 E.0.2 E.0.3 W.1.0 W.1.1 T.1.0 W.1.2 W.1.3 T.1.1 W.3.0 W.3.1 SG.0.0 SG.0.1 SG.0.2 SG.0.3
-            CP.0.0 AQ.0.0 EP.1.0 EP.1.1 M.0.0 EP.1.2 X.1.0 EP.1.3 W.3.2 X.1.1 MQ.1.0 EP.3.0 E.1.0 EP.3.1 E.1.1 EP.3.2
-            E.1.2 EP.3.3 E.1.3 W.3.3 SG.1.0 SG.1.1 SG.1.2 SG.1.3 E.3.0 E.3.1 E.3.2 E.3.3 EP.2.0 EP.2.1 EP.2.2 EP.2.3
-            NP.0.0 E.2.0 MP.1.0 W.2.0 E.2.1 NP.0.1 E.2.2 E.2.3 N.0.0 CP.1.0 NP.0.2 W.2.1 AQ.1.0 GM.0.0 N.0.1 T.2.0
-            Q.0.0 NP.0.3 W.2.2 W.2.3 M.1.0 T.2.1 SG.3.0 SG.3.1 SG.3.2 SG.3.3 CP.3.0 GM.0.1 N.0.2 SG.2.0 SG.2.1 SG.2.2
-            SG.2.3 CP.2.0 AQ.2.0 GM.0.2 N.0.3 AQ.3.0 V1.0.0 GM.1.0 V1.0.1 GM.0.3 V1.0.2 BT.0.0 V1.1.0 GM.1.1 V1.0.3 BT.0.1
-            V2.0.0 GM.1.2 Q.0.1 X.2.0 X.2.1 MQ.2.0 EP.5.0 Q.0.2 EP.5.1 EP.5.2 Q.0.3 EP.5.3 V1.1.1 BT.0.2 T.3.0 V3.0.0
-            E.5.0 T.3.1 V2.0.1 BT.0.3 V1.1.2 BT.1.0 V2.0.2 GM.1.3 V3.0.1 SG.5.0 E.5.1 SG.5.1 E.5.2 SG.5.2 E.5.3 SG.5.3
-            EP.4.0 EP.4.1 EP.4.2 X.3.0 EP.4.3 V3.0.2 V2.0.3 BT.1.1 CP.5.0 X.3.1 MQ.3.0 EP.6.0 E.4.0 EP.6.1 E.4.1 EP.6.2
-            E.4.2 EP.6.3 SG.4.0 SG.4.1 SG.4.2 E.4.3 SG.4.3 CP.4.0 V3.0.3 NP.1.0 V2.1.0 BT.1.2 V1.1.3 BT.1.3 E.6.0 E.6.1
-            E.6.2 E.6.3 NP.1.1 AQ.4.0 AQ.5.0 V2.1.1 GM.2.0 N.1.0 OP.0.0 NP.1.2 OP.0.1 V3.1.0 V2.1.2 BT.2.0 Q.1.0 OP.0.2
-            V2.1.3 GM.2.1 N.1.1 Q.1.1 OP.0.3 V3.1.1 V1.2.0 BT.2.1 O.0.0 EP.7.0 N.1.2 Q.1.2 EP.7.1 O.0.1 EP.7.2 O.0.2
-            EP.7.3 O.0.3 NP.1.3 V3.1.2 SG.6.0 SG.6.1 SG.6.2 SG.6.3 CP.6.0 V2.2.0 GM.2.2 V1.2.1 BT.2.2 V3.1.3 E.7.0 OP.1.0
-            E.7.1 E.7.2 E.7.3 OP.1.1 V2.2.1 BT.2.3 V1.2.2 GM.2.3 OP.1.2 SG.7.0 SG.7.1 SG.7.2 SG.7.3 CP.7.0 N.1.3 OP.1.3
-            V1.2.3 V2.2.2 V3.2.0 Q.1.3 OP.2.0 O.1.0 V3.2.1 OP.2.1 V2.2.3 O.1.1 V3.2.2 OP.2.2 O.1.2 V3.2.3 OP.2.3 O.1.3
-            AQ.6.0 AQ.7.0 GM.3.0 V1.3.0 BT.3.0 V2.3.0 GM.3.1 V1.3.1 BT.3.1 V2.3.1 GM.3.2 V1.3.2 BT.3.2 V2.3.2 O.2.0 O.2.1
-            GM.3.3 V1.3.3 BT.3.3 V2.3.3 O.2.2 O.2.3 V3.3.0 V3.3.1 V3.3.2 V3.3.3 OP.3.0 OP.3.1 OP.3.2 OP.3.3 O.3.0 O.3.1
+            W.0.0 W.0.1 W.0.2 W.0.3 T.0.0 X.0.0 T.0.1 X.0.1 MP.0.0 P.0.0 P.0.1 MQ.0.0 EP.1.0 EP.1.1 EP.1.2 EP.1.3
+            M.0.0 W.1.0 W.1.1 W.1.2 W.2.0 W.1.3 W.2.1 W.2.2 W.2.3 E.1.0 E.1.1 E.1.2 E.1.3 SG.1.0 SG.1.1 SG.1.2
+            SG.1.3 CP.1.0 EP.0.0 E.0.0 SG.0.0 EP.0.1 E.0.1 SG.0.1 EP.0.2 E.0.2 SG.0.2 EP.0.3 E.0.3 SG.0.3 CP.0.0 AQ.0.0
+            T.1.0 X.1.0 T.1.1 X.1.1 MQ.1.0 NP.0.0 W.3.0 NP.0.1 W.3.1 AQ.1.0 MP.1.0 NP.0.2 W.3.2 W.3.3 EP.2.0 N.0.0
+            Q.0.0 NP.0.3 N.0.1 Q.0.1 EP.2.1 GM.0.0 V1.0.0 GM.0.1 V1.0.1 GM.0.2 N.0.2 V1.0.2 GM.0.3 N.0.3 V1.0.3 BT.0.0
+            V2.0.0 BT.0.1 V2.0.1 M.1.0 EP.2.2 V3.0.0 BT.0.2 Q.0.2 V2.0.2 BT.0.3 Q.0.3 V2.0.3 EP.2.3 E.2.0 SG.2.0 E.2.1
+            SG.2.1 E.2.2 SG.2.2 E.2.3 SG.2.3 CP.2.0 T.2.0 X.2.0 T.2.1 X.2.1 MQ.2.0 EP.3.0 T.3.0 EP.3.1 X.3.0 EP.3.2
+            V3.0.1 T.3.1 E.3.0 EP.3.3 X.3.1 EP.5.0 E.3.1 EP.5.1 E.3.2 EP.5.2 EP.5.3 E.3.3 OP.0.0 E.5.0 OP.0.1 V3.0.2
+            E.5.1 OP.0.2 V3.0.3 E.5.2 OP.0.3 O.0.0 E.5.3 EP.4.0 AQ.2.0 SG.3.0 SG.3.1 SG.3.2 SG.3.3 CP.3.0 AQ.3.0 GM.1.0
+            O.0.1 EP.4.1 SG.5.0 SG.5.1 SG.5.2 SG.5.3 GM.1.1 EP.4.2 GM.1.2 O.0.2 EP.4.3 V1.1.0 GM.1.3 O.0.3 MQ.3.0 EP.6.0
+            E.4.0 EP.6.1 E.4.1 EP.6.2 V1.1.1 BT.1.0 E.4.2 EP.6.3 E.4.3 NP.1.0 V1.1.2 BT.1.1 E.6.0 NP.1.1 E.6.1 NP.1.2
+            CP.5.0 V1.1.3 BT.1.2 E.6.2 NP.1.3 N.1.0 SG.4.0 SG.4.1 SG.4.2 SG.4.3 CP.4.0 AQ.4.0 AQ.5.0 V2.1.0 GM.2.0 SG.6.0
+            SG.6.1 SG.6.2 E.6.3 SG.6.3 CP.6.0 V2.1.1 GM.2.1 N.1.1 V2.1.2 GM.2.2 V1.2.0 BT.1.3 V1.2.1 GM.2.3 N.1.2 N.1.3
+            V1.2.2 BT.2.0 EP.7.0 Q.1.0 EP.7.1 Q.1.1 EP.7.2 Q.1.2 EP.7.3 V2.1.3 BT.2.1 V1.2.3 BT.2.2 V2.2.0 BT.2.3 E.7.0
+            E.7.1 V3.1.0 Q.1.3 OP.1.0 E.7.2 E.7.3 V3.1.1 OP.1.1 AQ.6.0 V3.1.2 OP.1.2 V3.1.3 OP.1.3 O.1.0 O.1.1 O.1.2
+            O.1.3 SG.7.0 SG.7.1 SG.7.2 SG.7.3 CP.7.0 AQ.7.0 V2.2.1 GM.3.0 V2.2.2 GM.3.1 V2.2.3 GM.3.2 V1.3.0 GM.3.3 V1.3.1
+            BT.3.0 V1.3.2 BT.3.1 V3.2.0 OP.2.0 V3.2.1 OP.2.1 V1.3.3 BT.3.2 V3.2.2 OP.2.2 V3.2.3 OP.2.3 O.2.0 V2.3.0 BT.3.3
+            O.2.1 O.2.2 V2.3.1 V2.3.2 V2.3.3 O.2.3 V3.3.0 V3.3.1 OP.3.0 OP.3.1 V3.3.2 OP.3.2 V3.3.3 OP.3.3 O.3.0 O.3.1
             O.3.2 O.3.3
         """
         ctx.enter_context(tc.manual_schedule())

@@ -11,6 +11,7 @@ TILES = T // P
 CHUNK = 4
 COLS = CHUNK * P
 CB = C // P
+S_SHARE = {3: 128, 4: 128, 5: 128, 6: 128, 7: 128}
 
 F32 = mybir.dt.float32
 BF16 = mybir.dt.bfloat16
@@ -23,6 +24,36 @@ E2M1 = mybir.dt.float4_e2m1fn_x4
 ALU = mybir.AluOpType
 ACT = mybir.ActivationFunctionType
 
+VECTOR = """
+            W.0.0 W.0.1 W.0.2 W.0.3 P.0.0 MQ.0.0 P.0.1 W.1.0 W.1.1 W.3.1 SG.1.2 W.2.0 SG.1.0 SG.0.3
+            SG.0.0 W.3.0 SG.1.1 SG.1.3 W.2.1 CP.1.0 SG.0.1 AQ.1.0 SG.0.2 CP.0.0 MQ.1.0 AQ.0.0 V1.0.2 V1.0.0
+            V2.0.2 V2.0.0 V3.0.2 V3.0.0 SG.2.1 SG.2.0 SG.2.2 MQ.2.0 SG.2.3 V1.0.1 V1.0.3 SG.3.3 CP.2.0 SG.3.1
+            SG.3.2 SG.3.0 AQ.2.0 SG.5.0 CP.3.0 AQ.3.0 MQ.3.0 V2.0.1 V2.0.3 V3.0.1 V3.0.3 SG.5.3 SG.4.0 V1.1.0
+            SG.4.1 SG.4.3 V1.1.1 SG.5.2 SG.4.2 SG.5.1 CP.5.0 V2.1.0 CP.4.0 AQ.5.0 V1.1.3 SG.6.0 AQ.4.0 SG.6.1
+            V2.1.1 V2.1.3 SG.6.2 SG.6.3 V3.1.3 V1.1.2 V3.1.0 V1.2.0 V2.1.2 V3.1.1 V1.2.2 V3.1.2 CP.6.0 V2.2.0
+            SG.7.0 SG.7.3 SG.7.1 V2.2.2 V1.2.1 SG.7.2 V1.2.3 AQ.6.0 CP.7.0 V2.2.3 AQ.7.0 V3.2.3 V2.2.1 V3.2.2
+            V3.2.0 V1.3.1 V1.3.0 V3.2.1 V2.3.1 V1.3.3 V1.3.2 V2.3.3 V2.3.2 V3.3.4 V3.3.2 V2.3.0 V3.3.1 V3.3.0
+            V3.3.3
+"""
+SCALAR = """
+            X.0.0 X.0.1 E.0.0 M.0.0 E.0.3 E.1.0 E.0.1 E.1.3 E.1.2 E.0.2 X.1.0 N.0.0 E.1.1 Q.0.1
+            N.0.1 Q.0.0 Q.0.2 M.1.0 X.1.1 N.0.2 Q.0.3 N.0.3 E.2.0 X.2.1 E.2.3 E.2.1 E.2.2 X.2.0
+            E.3.0 E.3.3 E.3.2 E.4.0 E.3.1 E.5.0 X.3.0 X.3.1 CS.3.0 E.4.2 O.0.0 E.4.1 E.5.3 O.0.2
+            E.4.3 E.5.2 E.6.0 E.5.1 E.6.3 O.0.1 E.6.1 CS.5.0 O.0.3 CS.4.0 E.6.2 Q.1.1 N.1.2 N.1.0
+            Q.1.0 E.7.0 N.1.1 Q.1.2 E.7.3 E.7.1 E.7.2 N.1.3 CS.6.0 Q.1.3 CS.7.0 O.1.0 O.1.3 O.2.3
+            O.2.0 O.2.2 O.1.2 O.1.1 O.2.1 O.3.4 O.3.2 O.3.1 O.3.0 O.3.3
+"""
+TENSOR = """
+            T.0.0 T.0.1 MP.0.0 EP.0.0 EP.0.3 EP.1.0 EP.0.1 EP.1.3 EP.1.2 EP.0.2 EP.1.1 T.1.0 NP.0.0 NP.0.1
+            MP.1.0 NP.0.2 T.1.1 NP.0.3 T.2.1 EP.2.3 GM.0.2 GM.0.0 EP.2.0 BT.0.2 EP.2.1 BT.0.0 EP.2.2 GM.0.1
+            T.2.0 EP.3.3 EP.3.0 EP.3.2 GM.0.3 BT.0.3 EP.5.0 EP.4.0 EP.3.1 T.3.1 T.3.0 EP.4.2 OP.0.0 BT.0.1
+            EP.4.1 OP.0.2 EP.5.2 EP.5.3 EP.4.3 GM.1.0 EP.6.0 GM.1.1 EP.5.1 EP.6.3 EP.6.1 OP.0.1 BT.1.0 EP.6.2
+            OP.0.3 NP.1.0 GM.1.3 BT.1.1 NP.1.1 NP.1.2 BT.1.3 EP.7.1 EP.7.0 GM.1.2 GM.2.0 GM.2.2 BT.1.2 EP.7.3
+            EP.7.2 BT.2.0 BT.2.2 GM.2.1 NP.1.3 OP.1.0 GM.2.3 BT.2.1 OP.1.2 BT.2.3 OP.1.3 GM.3.0 OP.2.3 GM.3.1
+            BT.3.1 OP.2.2 OP.2.0 GM.3.3 GM.3.2 BT.3.3 BT.3.2 OP.1.1 BT.3.0 OP.3.4 OP.2.1 OP.3.2 OP.3.1 OP.3.0
+            OP.3.3
+"""
+
 
 def tile_spademodulationpointwise_w4_kernel(
     tc, x, m_bytes, m_scale, wm_words, wm_scales, bm, g, wg_words, wg_scales, wb_words, wb_scales, out
@@ -33,62 +64,63 @@ def tile_spademodulationpointwise_w4_kernel(
         mpool = ctx.enter_context(tc.tile_pool(name="mpool", bufs=4))
         apool = ctx.enter_context(tc.tile_pool(name="apool", bufs=4))
         qpool = ctx.enter_context(tc.tile_pool(name="qpool", bufs=4))
-        xpool = ctx.enter_context(tc.tile_pool(name="xpool", bufs=6))
-        ypool = ctx.enter_context(tc.tile_pool(name="ypool", bufs=3))
+        xpool = ctx.enter_context(tc.tile_pool(name="xpool", bufs=8))
+        ypool = ctx.enter_context(tc.tile_pool(name="ypool", bufs=6))
         ps_s = ctx.enter_context(tc.psum_pool(name="ps_s", bufs=5))
         ps_gb = ctx.enter_context(tc.psum_pool(name="ps_gb", bufs=3))
 
+        wm_sc_raw = keep.tile([P, K], U8, name="wm_sc_raw")
+        nc.vector.memset(wm_sc_raw[:].bitcast(I32), 0)
         ident_f = keep.tile([P, P], F32, name="ident_f")
         ident_b = keep.tile([P, P], BF16, name="ident_b")
         ones = keep.tile([P, 1], BF16, name="ones")
         minus_half = keep.tile([P, 1], F32, name="minus_half")
-        wm_sc_raw = keep.tile([P, K], U8, name="wm_sc_raw")
         wgb_sc = keep.tile([P, 4, C], U8, name="wgb_sc", align_bytes=64)
-        nc.vector.memset(wm_sc_raw[:].bitcast(I32), 0)
         make_identity(nc, ident_f[:])
         nc.gpsimd.tensor_copy(out=ident_b[:], in_=ident_f[:])
         nc.gpsimd.memset(ones[:], 1.0)
         nc.gpsimd.memset(wgb_sc[:].rearrange("p a n -> p (a n)").bitcast(I32), 0)
         nc.gpsimd.memset(minus_half[:], -0.5)
 
-        scale_bc = keep.tile([P, S], F32, name="scale_bc")
         scale_col = keep.tile([P, 4], F32, name="scale_col")
-        nc.scalar.dma_start(out=scale_col[:], in_=m_scale.rearrange("a o (p j) -> p (a o j)", j=4))
         b_raw = keep.tile([P, 2, 4], BF16, name="b_raw")
         g_raw = keep.tile([P, 2, 4], BF16, name="g_raw")
+        nc.scalar.dma_start(out=scale_col[:], in_=m_scale.rearrange("a o (p j) -> p (a o j)", j=4))
         nc.scalar.dma_start(out=b_raw[:], in_=bm.rearrange("(a p t) -> p a t", p=P, t=4))
         nc.scalar.dma_start(out=g_raw[:], in_=g.rearrange("(a p t) -> p a t", p=P, t=4))
+        scale_bc = keep.tile([P, 2, S], F32, name="scale_bc")
         scale_ps = ps_s.tile([P, 4, P], F32, tag="s", name="scale_ps")
         for j in range(4):
             nc.tensor.transpose(scale_ps[:, j, :], scale_col[:, j : j + 1].to_broadcast([P, P]), ident_f[:])
-        nc.scalar.copy(out=scale_bc[:].rearrange("p (k j) -> p k j", j=4), in_=scale_ps[:].rearrange("p j k -> p k j"))
+        for z in range(2):
+            nc.scalar.copy(out=scale_bc[:, z, :].rearrange("p (k j) -> p k j", j=4), in_=scale_ps[:].rearrange("p j k -> p k j"))
+
         m_u8 = []
         for c in range(4):
-            mt = keep.tile([P, CHUNK, S], U8, name="m_u8_%d" % c)
-            m_u8.append(mt)
+            m_u8_t = keep.tile([P, CHUNK, S], U8, name="m_u8_%d" % c)
+            m_u8.append(m_u8_t)
+        x_sb = []
+        for s in range(B):
+            x_t = keep.tile([P, TILES, C], BF16, name="x_sb_%d" % s)
+            x_sb.append(x_t)
+        wm_raw = keep.tile([P, 2 * K], U8, name="wm_raw")
+        wgb = keep.tile([P, 4, 2 * C], U8, name="wgb", align_bytes=64)
 
         def load_m(c):
             s, i0 = c // 2, (c % 2) * CHUNK
             nc.sync.dma_start(out=m_u8[c][:], in_=m_bytes[s].rearrange("(p i) k -> p i k", i=TILES)[:, i0 : i0 + CHUNK, :])
 
-        x_sb = []
-        for s in range(B):
-            xt = keep.tile([P, TILES, C], BF16, name="x_sb_%d" % s)
-            x_sb.append(xt)
-
         def load_x(s):
             nc.sync.dma_start(out=x_sb[s][:], in_=x[s].rearrange("(p i) c -> p i c", i=TILES))
-
-        wm_raw = keep.tile([P, 2 * K], U8, name="wm_raw")
-        wgb = keep.tile([P, 4, 2 * C], U8, name="wgb", align_bytes=64)
 
         for q in range(4):
             nc.sync.dma_start(out=wm_sc_raw[32 * q : 32 * q + 4, :].bitcast(I32), in_=wm_scales[0, 4 * q : 4 * q + 4, :].bitcast(I32))
         load_m(0)
         nc.sync.dma_start(out=wm_raw[:], in_=wm_words[0])
-        load_m(1)
         load_x(0)
+        load_m(1)
         load_m(2)
+        load_m(3)
         for w, scales in ((0, wg_scales), (2, wb_scales)):
             for q in range(4):
                 nc.sync.dma_start(
@@ -97,7 +129,6 @@ def tile_spademodulationpointwise_w4_kernel(
                 )
         nc.sync.dma_start(out=wgb[:, 0:2, :], in_=wg_words.rearrange("a p n -> p a n"))
         nc.sync.dma_start(out=wgb[:, 2:4, :], in_=wb_words.rearrange("a p n -> p a n"))
-        load_m(3)
         load_x(1)
 
         sgn = keep.tile([P, 2, 4], F32, name="sgn")
@@ -111,49 +142,49 @@ def tile_spademodulationpointwise_w4_kernel(
         wm_w = keep.tile([P, 2, 4, 2 * P], U8, name="wm_w", align_bytes=64)
         wm_sc = keep.tile([P, 2, 4, P], U8, name="wm_sc", align_bytes=64)
 
-        def permute_wm(a):
+        def permute_wm(z, a):
             nc.vector.tensor_copy(
                 out=wm_w[:, a].rearrange("p t (m b) -> p t m b", b=2),
                 in_=wm_raw[:].rearrange("p (a m t b) -> p a t m b", a=2, t=4, b=2)[:, a],
             )
-            nc.vector.tensor_copy(
-                out=wm_sc[:, a], in_=wm_sc_raw[:].rearrange("p (a m t) -> p a t m", a=2, t=4)[:, a]
+            nc.vector.tensor_copy(out=wm_sc[:, a], in_=wm_sc_raw[:].rearrange("p (a m t) -> p a t m", a=2, t=4)[:, a])
+
+        m_bf, mbank, mgrp, mq, mqs = {}, {}, {}, {}, {}
+
+        def widen(c, j):
+            n = 1 if c == 0 else 2
+            if n * j % 2 == 0:
+                m_bf[c, n * j // 2] = mpool.tile([P, 2, S], BF16, tag="m_bf", name="m_bf_t", bufs=6)
+            t = m_bf[c, n * j // 2]
+            o = n * j % 2
+            nc.vector.tensor_tensor(
+                out=t[:, o : o + n, :].rearrange("p i k -> p (i k)"),
+                in0=m_u8[c][:, n * j : n * j + n, :].rearrange("p i k -> p (i k)").bitcast(F8),
+                in1=scale_bc[:, 0:n, :].rearrange("p i k -> p (i k)"),
+                op=ALU.mult,
             )
-
-        mq, mqs, mgrp, mbank = {}, {}, {}, {}
-
-        m_bf = {}
-
-        def widen(i):
-            c, j = divmod(i, CHUNK)
-            m_bf[i] = mpool.tile([P, S], BF16, tag="m_bf", name="m_bf_t", bufs=12)
-            nc.vector.tensor_tensor(out=m_bf[i][:], in0=m_u8[c][:, j, :].bitcast(F8), in1=scale_bc[:], op=ALU.mult)
-
-        mbank = {}
 
         def turn_pe(c, h):
             mbank[c, h] = ps_s.tile([P, 2, 2, P], F32, tag="s", name="mbank_t")
             for j in range(2):
-                words = m_bf[CHUNK * c + 2 * h + j][:].bitcast(F32)
+                words = m_bf[c, h][:, j, :].bitcast(F32)
                 for u in range(2):
                     nc.tensor.transpose(mbank[c, h][:, j, u, :], words[:, u : S // 2 : 2], ident_f[:])
 
         def turn_out(c, h):
-            if h == 0:
+            if c not in mgrp:
                 mgrp[c] = mpool.tile([P, CHUNK, P, 4], BF16, tag="m_grouped", name="m_grouped", bufs=3, align_bytes=64)
             nc.scalar.copy(
                 out=mgrp[c][:, 2 * h : 2 * h + 2].rearrange("p j r t -> p (j r t)").bitcast(F32).rearrange("p (j r u) -> p j r u", j=2, u=2),
                 in_=mbank[c, h][:].rearrange("p j u r -> p j r u"),
             )
 
-        def quant_m(c):
+        def quant_m(c, z):
             mq[c] = qpool.tile([P, COLS], U32, tag="mq", name="mq_t", align_bytes=64)
             mqs[c] = qpool.tile([P, COLS], U8, tag="mqs", name="mqs_t", align_bytes=64)
             nc.vector.quantize_mx(out=mq[c][:].bitcast(E4M3), scales=mqs[c][:], in_=mgrp[c][:].rearrange("p j r t -> p (j r t)"))
 
-        aq, aqs, planes, grouped = {}, {}, {}, {}
-
-        hbank = {}
+        hbank, planes, grouped, aq, aqs = {}, {}, {}, {}, {}
 
         def embed_pe(k, t):
             c, a = divmod(k, 2)
@@ -170,8 +201,8 @@ def tile_spademodulationpointwise_w4_kernel(
 
         def embed_out(k, t):
             a = k % 2
-            if t == 0:
-                planes[k] = apool.tile([P, 4, COLS], BF16, tag="planes", name="planes")
+            if k not in planes:
+                planes[k] = apool.tile([P, 4, COLS], BF16, tag="planes", name="planes_t")
             nc.scalar.activation(
                 out=planes[k][:, t, :], in_=hbank[k, t][:], func=ACT.Relu, bias=gb[:, a, t : t + 1], scale=gabs[:, a, t : t + 1]
             )
@@ -182,23 +213,28 @@ def tile_spademodulationpointwise_w4_kernel(
                 out=planes[k][:, t, :], in0=planes[k][:, t, :], scalar1=sgn[:, a, t : t + 1], scalar2=None, op0=ALU.mult
             )
 
-        def interleave(k, copy):
-            grouped[k] = apool.tile([P, COLS, 4], BF16, tag="a_grouped", name="a_grouped", align_bytes=64)
+        def interleave(k, n0, n1, copy):
+            if k not in grouped:
+                grouped[k] = apool.tile([P, COLS, 4], BF16, tag="a_grouped", name="a_grouped", align_bytes=64)
             copy(
-                out=grouped[k][:].rearrange("p (n i) t -> p n t i", i=4),
-                in_=planes[k][:].rearrange("p t (n i) -> p n t i", i=4),
+                out=grouped[k][:, n0:n1, :].rearrange("p (n i) t -> p n t i", i=4),
+                in_=planes[k][:, :, n0:n1].rearrange("p t (n i) -> p n t i", i=4),
             )
 
-        def quant_a(k):
+        def interleave_v(k, z):
+            interleave(k, S_SHARE.get(k, 0), COLS, nc.vector.tensor_copy)
+
+        def interleave_s(k, z):
+            interleave(k, 0, S_SHARE[k], nc.scalar.copy)
+
+        def quant_a(k, z):
             aq[k] = qpool.tile([P, COLS], U32, tag="aq", name="aq_t", align_bytes=64, bufs=6)
             aqs[k] = qpool.tile([P, COLS], U8, tag="aqs", name="aqs_t", align_bytes=64, bufs=6)
             nc.vector.quantize_mx(out=aq[k][:].bitcast(E4M3), scales=aqs[k][:], in_=grouped[k][:].rearrange("p n t -> p (n t)"))
 
-        neg_mu, xt_ps, xt, rstd = {}, {}, {}, {}
+        sums, neg_mu, xt_ps, xc, rstd = {}, {}, {}, {}, {}
 
-        sums = {}
-
-        def mean_pe(s):
+        def mean_pe(s, z):
             sums[s] = ps_s.tile([P, CB], F32, tag="s", name="sums_t")
             for cb in range(CB):
                 for i in range(TILES):
@@ -210,36 +246,34 @@ def tile_spademodulationpointwise_w4_kernel(
                         stop=(i == TILES - 1),
                     )
 
-        def mean_out(s):
-            neg_mu[s] = xpool.tile([P, CB], F32, tag="neg_mu", name="neg_mu")
+        def mean_out(s, z):
+            neg_mu[s] = xpool.tile([P, CB], F32, tag="neg_mu", name="neg_mu_t")
             nc.scalar.activation(out=neg_mu[s][:], in_=sums[s][:], func=ACT.Copy, scale=-1.0 / T)
-
-        def x_var(s, cb):
-            junk = xpool.tile([P, TILES, P], BF16, tag="junk", name="junk", bufs=1)
-            ss = xpool.tile([P, 1], F32, tag="ss", name="ss")
-            nc.scalar.activation(out=junk[:], in_=xt_ps[s, cb][:], func=ACT.Square, bias=neg_mu[s][:, cb : cb + 1], accum_out=ss[:])
-            rstd[s, cb] = xpool.tile([P, 1], F32, tag="rstd", name="rstd_t", bufs=8)
-            nc.gpsimd.tensor_scalar(out=ss[:], in0=ss[:], scalar1=1.0 / T, scalar2=1e-5, op0=ALU.mult, op1=ALU.add)
-            nc.gpsimd.tensor_tensor(out=rstd[s, cb][:], in0=ss[:], in1=minus_half[:], op=ALU.pow)
 
         def center_pe(s, cb):
             xt_ps[s, cb] = ps_s.tile([P, TILES, P], BF16, tag="s", name="xt_ps_t")
             for i in range(TILES):
                 nc.tensor.transpose(xt_ps[s, cb][:, i, :], x_sb[s][:, i, cb * P : (cb + 1) * P], ident_b[:])
 
-        def x_center(s, cb):
-            xt[s, cb] = xpool.tile([P, TILES, P], F32, tag="xt", name="xt_t", bufs=8)
-            nc.scalar.activation(out=xt[s, cb][:], in_=xt_ps[s, cb][:], func=ACT.Identity, bias=neg_mu[s][:, cb : cb + 1])
+        def center_out(s, cb):
+            xc[s, cb] = xpool.tile([P, TILES, P], F32, tag="xc", name="xc_t")
+            nc.scalar.activation(out=xc[s, cb][:], in_=xt_ps[s, cb][:], func=ACT.Identity, bias=neg_mu[s][:, cb : cb + 1])
 
-        gam, bet, t1s, ys, lks = {}, {}, {}, {}, {}
+        def variance(s, cb):
+            junk = xpool.tile([P, TILES, P], BF16, tag="junk", name="junk", bufs=1)
+            ss = xpool.tile([P, 1], F32, tag="ss", name="ss")
+            nc.scalar.activation(out=junk[:], in_=xt_ps[s, cb][:], func=ACT.Square, bias=neg_mu[s][:, cb : cb + 1], accum_out=ss[:])
+            rstd[s, cb] = xpool.tile([P, 1], F32, tag="rstd", name="rstd_t")
+            nc.gpsimd.tensor_scalar(out=ss[:], in0=ss[:], scalar1=1.0 / T, scalar2=1e-5, op0=ALU.mult, op1=ALU.add)
+            nc.gpsimd.tensor_tensor(out=rstd[s, cb][:], in0=ss[:], in1=minus_half[:], op=ALU.pow)
 
-        def project(u, w):
-            c, cb = divmod(u, CB)
-            bank = ps_gb.tile([P, COLS], F32, tag="gb", name="bank_gb")
-            (gam if w == 0 else bet)[u] = bank
+        gam, bet, t1s, ys, lks, obank = {}, {}, {}, {}, {}, {}
+
+        def project(c, cb, w, banks):
+            banks[c, cb] = ps_gb.tile([P, COLS], F32, tag="gb", name="banks_t")
             for a in range(2):
                 nc.tensor.matmul_mx(
-                    out=bank[:],
+                    out=banks[c, cb][:],
                     lhsT=wgb[:, w + a, 2 * P * cb : 2 * P * (cb + 1)].bitcast(E2M1),
                     lhsT_scale=wgb_sc[:, w + a, P * cb : P * (cb + 1)],
                     rhs=aq[2 * c + a][:].bitcast(E4M3),
@@ -248,77 +282,103 @@ def tile_spademodulationpointwise_w4_kernel(
                     stop=(a == 1),
                 )
 
-        def modulate(u):
-            c, cb = divmod(u, CB)
+        def modulate(c, cb):
             s, i0 = c // 2, (c % 2) * CHUNK
-            t1s[u] = ypool.tile([P, COLS], F32, tag="t1", name="t1_t", bufs=6)
+            t1s[c, cb] = ypool.tile([P, COLS], F32, tag="t1", name="t1_t")
             nc.vector.scalar_tensor_tensor(
-                out=t1s[u][:], in0=gam[u][:], scalar=1.0, in1=xt[s, cb][:, i0 : i0 + CHUNK, :].rearrange("p i r -> p (i r)"), op0=ALU.add, op1=ALU.mult
+                out=t1s[c, cb][:],
+                in0=gam[c, cb][:],
+                scalar=1.0,
+                in1=xc[s, cb][:, i0 : i0 + CHUNK, :].rearrange("p i r -> p (i r)"),
+                op0=ALU.add,
+                op1=ALU.mult,
             )
 
-        def shift(u):
-            c, cb = divmod(u, CB)
-            ys[u] = ypool.tile([P, COLS], F32, tag="y", name="y_t", bufs=6)
+        def shift(c, cb):
+            ys[c, cb] = ypool.tile([P, COLS], F32, tag="y", name="y_t")
             nc.vector.scalar_tensor_tensor(
-                out=ys[u][:], in0=t1s[u][:], scalar=rstd[c // 2, cb][:], in1=bet[u][:], op0=ALU.mult, op1=ALU.add
+                out=ys[c, cb][:], in0=t1s[c, cb][:], scalar=rstd[c // 2, cb][:], in1=bet[c, cb][:], op0=ALU.mult, op1=ALU.add
             )
 
-        def leaky(u):
-            lks[u] = ypool.tile([P, CHUNK, P], F32, tag="lk", name="lk_t", bufs=6)
+        def span(c, cb):
+            return (cb, 0, CHUNK) if (c, cb) not in ((3, 3), (3, 4)) else (3, 2 * (cb - 3), 2 * (cb - 2))
+
+        def leaky(c, b):
+            cb, i0, i1 = span(c, b)
+            y = ys[c, cb][:, i0 * P : i1 * P]
+            lks[c, b] = ypool.tile([P, CHUNK, P], F32, tag="lk", name="lk_t")
             nc.vector.scalar_tensor_tensor(
-                out=lks[u][:].rearrange("p i r -> p (i r)"), in0=ys[u][:], scalar=0.2, in1=ys[u][:], op0=ALU.mult, op1=ALU.max
+                out=lks[c, b][:, 0 : i1 - i0, :].rearrange("p i r -> p (i r)"), in0=y, scalar=0.2, in1=y, op0=ALU.mult, op1=ALU.max
             )
 
-        obank = {}
+        def out_pe(c, b):
+            cb, i0, i1 = span(c, b)
+            obank[c, b] = ps_s.tile([P, CHUNK, P], F32, tag="s", name="obank_t")
+            for i in range(i1 - i0):
+                nc.tensor.transpose(obank[c, b][:, i, :], lks[c, b][:, i, :], ident_f[:])
 
-        def out_pe(u):
-            obank[u] = ps_s.tile([P, CHUNK, P], F32, tag="s", name="obank_t")
-            for i in range(CHUNK):
-                nc.tensor.transpose(obank[u][:, i, :], lks[u][:, i, :], ident_f[:])
-
-        def out_store(u):
-            c, cb = divmod(u, CB)
-            s, i0 = c // 2, (c % 2) * CHUNK
-            res = ypool.tile([P, CHUNK, P], F32, tag="res", name="res_t", bufs=6)
-            nc.scalar.copy(out=res[:], in_=obank[u][:])
+        def out_store(c, b):
+            cb, i0, i1 = span(c, b)
+            s, j0 = c // 2, (c % 2) * CHUNK
+            res = ypool.tile([P, CHUNK, P], F32, tag="res", name="res_t")
+            nc.scalar.copy(out=res[:, 0 : i1 - i0, :], in_=obank[c, b][:, 0 : i1 - i0, :])
             nc.sync.dma_start(
-                out=out[s].rearrange("(p i) c -> p i c", i=TILES)[:, i0 : i0 + CHUNK, cb * P : (cb + 1) * P], in_=res[:]
+                out=out[s].rearrange("(p i) c -> p i c", i=TILES)[:, j0 + i0 : j0 + i1, cb * P : (cb + 1) * P],
+                in_=res[:, 0 : i1 - i0, :],
             )
 
         calls = {
-            "W": lambda c, j: widen(CHUNK * c + j),
-            "P": lambda z, a: permute_wm(a),
-            "T": turn_pe, "X": turn_out, "MQ": lambda c, z: quant_m(c),
-            "EP": embed_pe, "E": embed_out, "SG": apply_sign,
-            "CP": lambda k, z: interleave(k, nc.vector.tensor_copy), "AQ": lambda k, z: quant_a(k),
-            "MP": lambda s, z: mean_pe(s), "M": lambda s, z: mean_out(s),
-            "NP": center_pe, "N": x_center, "Q": x_var, "G": lambda s, b: None,
-            "GM": lambda c, b: project(CB * c + b, 0), "BT": lambda c, b: project(CB * c + b, 2),
-            "V1": lambda c, b: modulate(CB * c + b), "V2": lambda c, b: shift(CB * c + b), "V3": lambda c, b: leaky(CB * c + b),
-            "OP": lambda c, b: out_pe(CB * c + b), "O": lambda c, b: out_store(CB * c + b),
+            "W": widen, "P": permute_wm, "T": turn_pe, "X": turn_out, "MQ": quant_m,
+            "EP": embed_pe, "E": embed_out, "SG": apply_sign, "CP": interleave_v, "CS": interleave_s, "AQ": quant_a,
+            "MP": mean_pe, "M": mean_out, "NP": center_pe, "N": center_out, "Q": variance,
+            "GM": lambda c, b: project(c, b, 0, gam), "BT": lambda c, b: project(c, b, 2, bet),
+            "V1": modulate, "V2": shift, "V3": leaky, "OP": out_pe, "O": out_store,
         }
-        order = """
-            W.0.0 W.0.1 W.0.2 W.0.3 T.0.0 X.0.0 T.0.1 X.0.1 MP.0.0 P.0.0 P.0.1 MQ.0.0 EP.1.0 EP.1.1 EP.1.2 EP.1.3
-            M.0.0 W.1.0 W.1.1 W.1.2 W.2.0 W.1.3 W.2.1 W.2.2 W.2.3 E.1.0 E.1.1 E.1.2 E.1.3 SG.1.0 SG.1.1 SG.1.2
-            SG.1.3 CP.1.0 EP.0.0 E.0.0 SG.0.0 EP.0.1 E.0.1 SG.0.1 EP.0.2 E.0.2 SG.0.2 EP.0.3 E.0.3 SG.0.3 CP.0.0 AQ.0.0
-            T.1.0 X.1.0 T.1.1 X.1.1 MQ.1.0 NP.0.0 W.3.0 NP.0.1 W.3.1 AQ.1.0 MP.1.0 NP.0.2 W.3.2 W.3.3 EP.2.0 N.0.0
-            Q.0.0 NP.0.3 N.0.1 Q.0.1 EP.2.1 GM.0.0 V1.0.0 GM.0.1 V1.0.1 GM.0.2 N.0.2 V1.0.2 GM.0.3 N.0.3 V1.0.3 BT.0.0
-            V2.0.0 BT.0.1 V2.0.1 M.1.0 EP.2.2 V3.0.0 BT.0.2 Q.0.2 V2.0.2 BT.0.3 Q.0.3 V2.0.3 EP.2.3 E.2.0 SG.2.0 E.2.1
-            SG.2.1 E.2.2 SG.2.2 E.2.3 SG.2.3 CP.2.0 T.2.0 X.2.0 T.2.1 X.2.1 MQ.2.0 EP.3.0 T.3.0 EP.3.1 X.3.0 EP.3.2
-            V3.0.1 T.3.1 E.3.0 EP.3.3 X.3.1 EP.5.0 E.3.1 EP.5.1 E.3.2 EP.5.2 EP.5.3 E.3.3 OP.0.0 E.5.0 OP.0.1 V3.0.2
-            E.5.1 OP.0.2 V3.0.3 E.5.2 OP.0.3 O.0.0 E.5.3 EP.4.0 AQ.2.0 SG.3.0 SG.3.1 SG.3.2 SG.3.3 CP.3.0 AQ.3.0 GM.1.0
-            O.0.1 EP.4.1 SG.5.0 SG.5.1 SG.5.2 SG.5.3 GM.1.1 EP.4.2 GM.1.2 O.0.2 EP.4.3 V1.1.0 GM.1.3 O.0.3 MQ.3.0 EP.6.0
-            E.4.0 EP.6.1 E.4.1 EP.6.2 V1.1.1 BT.1.0 E.4.2 EP.6.3 E.4.3 NP.1.0 V1.1.2 BT.1.1 E.6.0 NP.1.1 E.6.1 NP.1.2
-            CP.5.0 V1.1.3 BT.1.2 E.6.2 NP.1.3 N.1.0 SG.4.0 SG.4.1 SG.4.2 SG.4.3 CP.4.0 AQ.4.0 AQ.5.0 V2.1.0 GM.2.0 SG.6.0
-            SG.6.1 SG.6.2 E.6.3 SG.6.3 CP.6.0 V2.1.1 GM.2.1 N.1.1 V2.1.2 GM.2.2 V1.2.0 BT.1.3 V1.2.1 GM.2.3 N.1.2 N.1.3
-            V1.2.2 BT.2.0 EP.7.0 Q.1.0 EP.7.1 Q.1.1 EP.7.2 Q.1.2 EP.7.3 V2.1.3 BT.2.1 V1.2.3 BT.2.2 V2.2.0 BT.2.3 E.7.0
-            E.7.1 V3.1.0 Q.1.3 OP.1.0 E.7.2 E.7.3 V3.1.1 OP.1.1 AQ.6.0 V3.1.2 OP.1.2 V3.1.3 OP.1.3 O.1.0 O.1.1 O.1.2
-            O.1.3 SG.7.0 SG.7.1 SG.7.2 SG.7.3 CP.7.0 AQ.7.0 V2.2.1 GM.3.0 V2.2.2 GM.3.1 V2.2.3 GM.3.2 V1.3.0 GM.3.3 V1.3.1
-            BT.3.0 V1.3.2 BT.3.1 V3.2.0 OP.2.0 V3.2.1 OP.2.1 V1.3.3 BT.3.2 V3.2.2 OP.2.2 V3.2.3 OP.2.3 O.2.0 V2.3.0 BT.3.3
-            O.2.1 O.2.2 V2.3.1 V2.3.2 V2.3.3 O.2.3 V3.3.0 V3.3.1 OP.3.0 OP.3.1 V3.3.2 OP.3.2 V3.3.3 OP.3.3 O.3.0 O.3.1
-            O.3.2 O.3.3
-        """
+
+        def needs(name, a, b):
+            if name == "T":
+                return [("W", a, 2 * b), ("W", a, 2 * b + 1)] if a == 0 else [("W", a, b)]
+            if name == "X":
+                return [("T", a, b)]
+            if name == "MQ":
+                return [("X", a, 0), ("X", a, 1)]
+            if name == "EP":
+                return [("MQ", a // 2, 0), ("P", 0, a % 2)]
+            if name == "E":
+                return [("EP", a, b)]
+            if name == "SG":
+                return [("E", a, b)]
+            if name in ("CP", "CS"):
+                return [("SG", a, t) for t in range(4)]
+            if name == "AQ":
+                return [("CP", a, 0)] + ([("CS", a, 0)] if a in S_SHARE else [])
+            if name == "M":
+                return [("MP", a, 0)]
+            if name in ("N", "Q"):
+                return [("M", a, 0), ("NP", a, b)]
+            if name in ("GM", "BT"):
+                return [("AQ", 2 * a, 0), ("AQ", 2 * a + 1, 0)]
+            if name == "V1":
+                return [("GM", a, b), ("N", a // 2, b)]
+            if name == "V2":
+                return [("V1", a, b), ("BT", a, b), ("Q", a // 2, b)]
+            if name == "V3":
+                return [("V2", a, span(a, b)[0])]
+            if name == "OP":
+                return [("V3", a, b)]
+            if name == "O":
+                return [("OP", a, b)]
+            return []
+
         ctx.enter_context(tc.manual_schedule())
-        for word in order.split():
-            name, a, b = word.split(".")
-            calls[name](int(a), int(b))
+        queues = []
+        for text in (VECTOR, SCALAR, TENSOR):
+            words = [w.split(".") for w in text.split()]
+            queues.append([(w[0], int(w[1]), int(w[2])) for w in words])
+        written = set()
+        while any(queues):
+            for queue in queues:
+                while queue and all(n in written for n in needs(*queue[0])):
+                    call = queue.pop(0)
+                    calls[call[0]](call[1], call[2])
+                    written.add(call)

@@ -11,7 +11,7 @@ TILES = T // P
 CHUNK = 4
 COLS = CHUNK * P
 CB = C // P
-S_SHARE = {3: 128, 4: 128, 5: 128, 6: 128, 7: 128}
+S_SHARE = {}
 
 F32 = mybir.dt.float32
 BF16 = mybir.dt.bfloat16
@@ -25,33 +25,33 @@ ALU = mybir.AluOpType
 ACT = mybir.ActivationFunctionType
 
 VECTOR = """
-            W.0.0 W.0.1 W.0.2 W.0.3 P.0.0 MQ.0.0 P.0.1 W.1.0 W.1.1 W.3.1 SG.1.2 W.2.0 SG.1.0 SG.0.3
-            SG.0.0 W.3.0 SG.1.1 SG.1.3 W.2.1 CP.1.0 SG.0.1 AQ.1.0 SG.0.2 CP.0.0 MQ.1.0 AQ.0.0 V1.0.2 V1.0.0
-            V2.0.2 V2.0.0 V3.0.2 V3.0.0 SG.2.1 SG.2.0 SG.2.2 MQ.2.0 SG.2.3 V1.0.1 V1.0.3 SG.3.3 CP.2.0 SG.3.1
-            SG.3.2 SG.3.0 AQ.2.0 SG.5.0 CP.3.0 AQ.3.0 MQ.3.0 V2.0.1 V2.0.3 V3.0.1 V3.0.3 SG.5.3 SG.4.0 V1.1.0
-            SG.4.1 SG.4.3 V1.1.1 SG.5.2 SG.4.2 SG.5.1 CP.5.0 V2.1.0 CP.4.0 AQ.5.0 V1.1.3 SG.6.0 AQ.4.0 SG.6.1
-            V2.1.1 V2.1.3 SG.6.2 SG.6.3 V3.1.3 V1.1.2 V3.1.0 V1.2.0 V2.1.2 V3.1.1 V1.2.2 V3.1.2 CP.6.0 V2.2.0
-            SG.7.0 SG.7.3 SG.7.1 V2.2.2 V1.2.1 SG.7.2 V1.2.3 AQ.6.0 CP.7.0 V2.2.3 AQ.7.0 V3.2.3 V2.2.1 V3.2.2
-            V3.2.0 V1.3.1 V1.3.0 V3.2.1 V2.3.1 V1.3.3 V1.3.2 V2.3.3 V2.3.2 V3.3.4 V3.3.2 V2.3.0 V3.3.1 V3.3.0
-            V3.3.3
+            W.0.0 W.0.1 W.0.2 W.0.3 P.0.0 MQ.0.0 P.0.1 W.1.0 W.3.0 W.1.1 SG.1.0 SG.0.0 SG.0.3 SG.0.1
+            SG.1.3 SG.0.2 W.3.1 SG.1.1 SG.1.2 CP.0.0 CP.1.0 AQ.0.0 AQ.1.0 MQ.1.0 W.2.1 V1.0.2 V1.0.0 W.2.0
+            V2.0.0 V1.0.1 SG.2.0 V2.0.1 V1.0.3 V3.0.1 V2.0.2 V3.0.0 V3.0.2 SG.2.3 SG.2.1 SG.3.0 MQ.2.0 SG.2.2
+            V2.0.3 CP.2.0 SG.3.2 SG.3.3 SG.5.0 SG.3.1 AQ.2.0 CP.3.0 MQ.3.0 AQ.3.0 SG.5.1 SG.4.1 V3.0.3 SG.4.0
+            SG.5.3 SG.5.2 V1.1.1 CP.5.0 V1.1.3 SG.4.3 AQ.5.0 V1.1.2 SG.4.2 V2.1.3 CP.4.0 V2.1.1 SG.6.1 SG.7.2
+            V1.1.0 SG.6.3 V3.1.3 SG.6.0 SG.6.2 AQ.4.0 CP.6.0 V2.1.2 V2.1.0 SG.7.3 V3.1.2 V3.1.1 SG.7.0 V3.1.0
+            SG.7.1 V1.2.0 CP.7.0 V1.2.3 V1.2.1 AQ.7.0 V1.2.2 V2.2.0 V2.2.1 V3.2.0 AQ.6.0 V2.2.3 V2.2.2 V3.2.3
+            V1.3.0 V1.3.3 V3.2.2 V1.3.1 V1.3.2 V2.3.3 V3.2.1 V3.3.4 V3.3.3 V2.3.2 V2.3.1 V3.3.2 V2.3.0 V3.3.1
+            V3.3.0
 """
 SCALAR = """
-            X.0.0 X.0.1 E.0.0 M.0.0 E.0.3 E.1.0 E.0.1 E.1.3 E.1.2 E.0.2 X.1.0 N.0.0 E.1.1 Q.0.1
-            N.0.1 Q.0.0 Q.0.2 M.1.0 X.1.1 N.0.2 Q.0.3 N.0.3 E.2.0 X.2.1 E.2.3 E.2.1 E.2.2 X.2.0
-            E.3.0 E.3.3 E.3.2 E.4.0 E.3.1 E.5.0 X.3.0 X.3.1 CS.3.0 E.4.2 O.0.0 E.4.1 E.5.3 O.0.2
-            E.4.3 E.5.2 E.6.0 E.5.1 E.6.3 O.0.1 E.6.1 CS.5.0 O.0.3 CS.4.0 E.6.2 Q.1.1 N.1.2 N.1.0
-            Q.1.0 E.7.0 N.1.1 Q.1.2 E.7.3 E.7.1 E.7.2 N.1.3 CS.6.0 Q.1.3 CS.7.0 O.1.0 O.1.3 O.2.3
-            O.2.0 O.2.2 O.1.2 O.1.1 O.2.1 O.3.4 O.3.2 O.3.1 O.3.0 O.3.3
+            X.0.0 X.0.1 M.0.0 E.0.0 E.0.3 E.0.2 E.1.0 E.0.1 E.1.3 E.1.2 E.1.1 X.1.0 Q.0.2 X.1.1
+            N.0.0 N.0.2 Q.0.0 M.1.0 N.0.1 Q.0.1 N.0.3 E.2.0 Q.0.3 E.2.3 E.2.1 E.3.0 X.2.1 X.2.0
+            E.2.2 E.3.2 E.3.3 E.5.0 E.3.1 X.3.1 X.3.0 E.4.0 E.5.1 E.4.1 E.5.3 E.5.2 O.0.2 O.0.0
+            E.4.3 O.0.1 E.7.0 E.4.2 E.6.0 E.7.2 E.6.1 E.6.3 E.6.2 Q.1.0 E.7.3 E.7.1 Q.1.3 N.1.0
+            N.1.3 N.1.1 N.1.2 Q.1.1 Q.1.2 O.0.3 O.1.2 O.2.0 O.1.1 O.1.3 O.1.0 O.2.3 O.2.2 O.2.1
+            O.3.3 O.3.4 O.3.2 O.3.1 O.3.0
 """
 TENSOR = """
-            T.0.0 T.0.1 MP.0.0 EP.0.0 EP.0.3 EP.1.0 EP.0.1 EP.1.3 EP.1.2 EP.0.2 EP.1.1 T.1.0 NP.0.0 NP.0.1
-            MP.1.0 NP.0.2 T.1.1 NP.0.3 T.2.1 EP.2.3 GM.0.2 GM.0.0 EP.2.0 BT.0.2 EP.2.1 BT.0.0 EP.2.2 GM.0.1
-            T.2.0 EP.3.3 EP.3.0 EP.3.2 GM.0.3 BT.0.3 EP.5.0 EP.4.0 EP.3.1 T.3.1 T.3.0 EP.4.2 OP.0.0 BT.0.1
-            EP.4.1 OP.0.2 EP.5.2 EP.5.3 EP.4.3 GM.1.0 EP.6.0 GM.1.1 EP.5.1 EP.6.3 EP.6.1 OP.0.1 BT.1.0 EP.6.2
-            OP.0.3 NP.1.0 GM.1.3 BT.1.1 NP.1.1 NP.1.2 BT.1.3 EP.7.1 EP.7.0 GM.1.2 GM.2.0 GM.2.2 BT.1.2 EP.7.3
-            EP.7.2 BT.2.0 BT.2.2 GM.2.1 NP.1.3 OP.1.0 GM.2.3 BT.2.1 OP.1.2 BT.2.3 OP.1.3 GM.3.0 OP.2.3 GM.3.1
-            BT.3.1 OP.2.2 OP.2.0 GM.3.3 GM.3.2 BT.3.3 BT.3.2 OP.1.1 BT.3.0 OP.3.4 OP.2.1 OP.3.2 OP.3.1 OP.3.0
-            OP.3.3
+            T.0.0 T.0.1 MP.0.0 EP.0.0 EP.0.3 EP.0.2 EP.1.0 EP.0.1 EP.1.3 EP.1.1 T.1.0 EP.1.2 T.1.1 NP.0.2
+            NP.0.0 MP.1.0 NP.0.1 NP.0.3 GM.0.2 GM.0.0 BT.0.0 GM.0.1 EP.2.0 EP.2.3 EP.2.1 EP.3.0 BT.0.1 GM.0.3
+            BT.0.2 T.2.1 T.2.0 EP.2.2 EP.3.3 EP.3.2 BT.0.3 EP.3.1 EP.5.0 T.3.1 T.3.0 EP.4.0 EP.5.1 EP.4.1
+            EP.5.3 EP.5.2 OP.0.2 OP.0.0 OP.0.1 GM.1.1 EP.4.3 GM.1.2 EP.7.0 GM.1.3 EP.4.2 EP.6.0 BT.1.3 EP.7.2
+            EP.6.2 EP.6.3 EP.6.1 BT.1.1 EP.7.3 GM.1.0 NP.1.0 BT.1.2 EP.7.1 BT.1.0 NP.1.3 NP.1.1 GM.2.0 GM.2.3
+            GM.2.1 OP.1.2 NP.1.2 OP.1.3 OP.0.3 GM.2.2 BT.2.0 BT.2.1 BT.2.3 BT.2.2 OP.1.0 OP.1.1 OP.2.0 GM.3.0
+            GM.3.3 GM.3.1 GM.3.2 BT.3.3 BT.3.2 BT.3.0 BT.3.1 OP.2.3 OP.2.2 OP.2.1 OP.3.4 OP.3.3 OP.3.2 OP.3.1
+            OP.3.0
 """
 
 

from contextlib import ExitStack

import concourse.mybir as mybir
from concourse.masks import make_identity

B, T, S, K, C = 2, 1024, 512, 1024, 512
FLOPS = 2 * B * T * (S * K + 2 * K * C)

P = 128
TILES = T // P
CHUNK = 4
COLS = CHUNK * P
CB = C // P
S_SHARE = {}

F32 = mybir.dt.float32
BF16 = mybir.dt.bfloat16
I32 = mybir.dt.int32
U32 = mybir.dt.uint32
U8 = mybir.dt.uint8
F8 = mybir.dt.float8_e4m3fn
E4M3 = mybir.dt.float8_e4m3fn_x4
E2M1 = mybir.dt.float4_e2m1fn_x4
ALU = mybir.AluOpType
ACT = mybir.ActivationFunctionType

VECTOR = """
            W.0.0 W.0.1 W.0.2 W.0.3 P.0.0 MQ.0.0 P.0.1 W.1.0 W.3.0 W.1.1 SG.1.0 SG.0.0 SG.0.3 SG.0.1
            SG.1.3 SG.0.2 W.3.1 SG.1.1 SG.1.2 CP.0.0 CP.1.0 AQ.0.0 AQ.1.0 MQ.1.0 W.2.1 V1.0.2 V1.0.0 W.2.0
            V2.0.0 V1.0.1 SG.2.0 V2.0.1 V1.0.3 V3.0.1 V2.0.2 V3.0.0 V3.0.2 SG.2.3 SG.2.1 SG.3.0 MQ.2.0 SG.2.2
            V2.0.3 CP.2.0 SG.3.2 SG.3.3 SG.5.0 SG.3.1 AQ.2.0 CP.3.0 MQ.3.0 AQ.3.0 SG.5.1 SG.4.1 V3.0.3 SG.4.0
            SG.5.3 SG.5.2 V1.1.1 CP.5.0 V1.1.3 SG.4.3 AQ.5.0 V1.1.2 SG.4.2 V2.1.3 CP.4.0 V2.1.1 SG.6.1 SG.7.2
            V1.1.0 SG.6.3 V3.1.3 SG.6.0 SG.6.2 AQ.4.0 CP.6.0 V2.1.2 V2.1.0 SG.7.3 V3.1.2 V3.1.1 SG.7.0 V3.1.0
            SG.7.1 V1.2.0 CP.7.0 V1.2.3 V1.2.1 AQ.7.0 V1.2.2 V2.2.0 V2.2.1 V3.2.0 AQ.6.0 V2.2.3 V2.2.2 V3.2.3
            V1.3.0 V1.3.3 V3.2.2 V1.3.1 V1.3.2 V2.3.3 V3.2.1 V3.3.4 V3.3.3 V2.3.2 V2.3.1 V3.3.2 V2.3.0 V3.3.1
            V3.3.0
"""
SCALAR = """
            X.0.0 X.0.1 M.0.0 E.0.0 E.0.3 E.0.2 E.1.0 E.0.1 E.1.3 E.1.2 E.1.1 X.1.0 Q.0.2 X.1.1
            N.0.0 N.0.2 Q.0.0 M.1.0 N.0.1 Q.0.1 N.0.3 E.2.0 Q.0.3 E.2.3 E.2.1 E.3.0 X.2.1 X.2.0
            E.2.2 E.3.2 E.3.3 E.5.0 E.3.1 X.3.1 X.3.0 E.4.0 E.5.1 E.4.1 E.5.3 E.5.2 O.0.2 O.0.0
            E.4.3 O.0.1 E.7.0 E.4.2 E.6.0 E.7.2 E.6.1 E.6.3 E.6.2 Q.1.0 E.7.3 E.7.1 Q.1.3 N.1.0
            N.1.3 N.1.1 N.1.2 Q.1.1 Q.1.2 O.0.3 O.1.2 O.2.0 O.1.1 O.1.3 O.1.0 O.2.3 O.2.2 O.2.1
            O.3.3 O.3.4 O.3.2 O.3.1 O.3.0
"""
TENSOR = """
            T.0.0 T.0.1 MP.0.0 EP.0.0 EP.0.3 EP.0.2 EP.1.0 EP.0.1 EP.1.3 EP.1.1 T.1.0 EP.1.2 T.1.1 NP.0.2
            NP.0.0 MP.1.0 NP.0.1 NP.0.3 GM.0.2 GM.0.0 BT.0.0 GM.0.1 EP.2.0 EP.2.3 EP.2.1 EP.3.0 BT.0.1 GM.0.3
            BT.0.2 T.2.1 T.2.0 EP.2.2 EP.3.3 EP.3.2 BT.0.3 EP.3.1 EP.5.0 T.3.1 T.3.0 EP.4.0 EP.5.1 EP.4.1
            EP.5.3 EP.5.2 OP.0.2 OP.0.0 OP.0.1 GM.1.1 EP.4.3 GM.1.2 EP.7.0 GM.1.3 EP.4.2 EP.6.0 BT.1.3 EP.7.2
            EP.6.2 EP.6.3 EP.6.1 BT.1.1 EP.7.3 GM.1.0 NP.1.0 BT.1.2 EP.7.1 BT.1.0 NP.1.3 NP.1.1 GM.2.0 GM.2.3
            GM.2.1 OP.1.2 NP.1.2 OP.1.3 OP.0.3 GM.2.2 BT.2.0 BT.2.1 BT.2.3 BT.2.2 OP.1.0 OP.1.1 OP.2.0 GM.3.0
            GM.3.3 GM.3.1 GM.3.2 BT.3.3 BT.3.2 BT.3.0 BT.3.1 OP.2.3 OP.2.2 OP.2.1 OP.3.4 OP.3.3 OP.3.2 OP.3.1
            OP.3.0
"""


def tile_spademodulationpointwise_w4_kernel(
    tc, x, m_bytes, m_scale, wm_words, wm_scales, bm, g, wg_words, wg_scales, wb_words, wb_scales, out
):
    nc = tc.nc
    with ExitStack() as ctx:
        keep = ctx.enter_context(tc.tile_pool(name="keep", bufs=1))
        mpool = ctx.enter_context(tc.tile_pool(name="mpool", bufs=4))
        apool = ctx.enter_context(tc.tile_pool(name="apool", bufs=4))
        qpool = ctx.enter_context(tc.tile_pool(name="qpool", bufs=4))
        xpool = ctx.enter_context(tc.tile_pool(name="xpool", bufs=8))
        ypool = ctx.enter_context(tc.tile_pool(name="ypool", bufs=6))
        ps_s = ctx.enter_context(tc.psum_pool(name="ps_s", bufs=5))
        ps_gb = ctx.enter_context(tc.psum_pool(name="ps_gb", bufs=3))

        wm_sc_raw = keep.tile([P, K], U8, name="wm_sc_raw")
        nc.vector.memset(wm_sc_raw[:].bitcast(I32), 0)
        ident_f = keep.tile([P, P], F32, name="ident_f")
        ident_b = keep.tile([P, P], BF16, name="ident_b")
        ones = keep.tile([P, 1], BF16, name="ones")
        minus_half = keep.tile([P, 1], F32, name="minus_half")
        wgb_sc = keep.tile([P, 4, C], U8, name="wgb_sc", align_bytes=64)
        make_identity(nc, ident_f[:])
        nc.gpsimd.tensor_copy(out=ident_b[:], in_=ident_f[:])
        nc.gpsimd.memset(ones[:], 1.0)
        nc.gpsimd.memset(wgb_sc[:].rearrange("p a n -> p (a n)").bitcast(I32), 0)
        nc.gpsimd.memset(minus_half[:], -0.5)

        scale_col = keep.tile([P, 4], F32, name="scale_col")
        b_raw = keep.tile([P, 2, 4], BF16, name="b_raw")
        g_raw = keep.tile([P, 2, 4], BF16, name="g_raw")
        nc.scalar.dma_start(out=scale_col[:], in_=m_scale.rearrange("a o (p j) -> p (a o j)", j=4))
        nc.scalar.dma_start(out=b_raw[:], in_=bm.rearrange("(a p t) -> p a t", p=P, t=4))
        nc.scalar.dma_start(out=g_raw[:], in_=g.rearrange("(a p t) -> p a t", p=P, t=4))
        scale_bc = keep.tile([P, 2, S], F32, name="scale_bc")
        scale_ps = ps_s.tile([P, 4, P], F32, tag="s", name="scale_ps")
        for j in range(4):
            nc.tensor.transpose(scale_ps[:, j, :], scale_col[:, j : j + 1].to_broadcast([P, P]), ident_f[:])
        for z in range(2):
            nc.scalar.copy(out=scale_bc[:, z, :].rearrange("p (k j) -> p k j", j=4), in_=scale_ps[:].rearrange("p j k -> p k j"))

        m_u8 = []
        for c in range(4):
            m_u8_t = keep.tile([P, CHUNK, S], U8, name="m_u8_%d" % c)
            m_u8.append(m_u8_t)
        x_sb = []
        for s in range(B):
            x_t = keep.tile([P, TILES, C], BF16, name="x_sb_%d" % s)
            x_sb.append(x_t)
        wm_raw = keep.tile([P, 2 * K], U8, name="wm_raw")
        wgb = keep.tile([P, 4, 2 * C], U8, name="wgb", align_bytes=64)

        def load_m(c):
            s, i0 = c // 2, (c % 2) * CHUNK
            nc.sync.dma_start(out=m_u8[c][:], in_=m_bytes[s].rearrange("(p i) k -> p i k", i=TILES)[:, i0 : i0 + CHUNK, :])

        def load_x(s):
            nc.sync.dma_start(out=x_sb[s][:], in_=x[s].rearrange("(p i) c -> p i c", i=TILES))

        for q in range(4):
            nc.sync.dma_start(out=wm_sc_raw[32 * q : 32 * q + 4, :].bitcast(I32), in_=wm_scales[0, 4 * q : 4 * q + 4, :].bitcast(I32))
        load_m(0)
        nc.sync.dma_start(out=wm_raw[:], in_=wm_words[0])
        load_x(0)
        load_m(1)
        load_m(2)
        load_m(3)
        for w, scales in ((0, wg_scales), (2, wb_scales)):
            for q in range(4):
                nc.sync.dma_start(
                    out=wgb_sc[32 * q : 32 * q + 4, w : w + 2, :].bitcast(I32),
                    in_=scales[:, 4 * q : 4 * q + 4, :].rearrange("a q n -> q a n").bitcast(I32),
                )
        nc.sync.dma_start(out=wgb[:, 0:2, :], in_=wg_words.rearrange("a p n -> p a n"))
        nc.sync.dma_start(out=wgb[:, 2:4, :], in_=wb_words.rearrange("a p n -> p a n"))
        load_x(1)

        sgn = keep.tile([P, 2, 4], F32, name="sgn")
        gabs = keep.tile([P, 2, 4], F32, name="gabs")
        gb = keep.tile([P, 2, 4], F32, name="gb")
        nc.gpsimd.tensor_scalar(out=sgn[:], in0=g_raw[:], scalar1=0.0, scalar2=2.0, op0=ALU.is_ge, op1=ALU.mult)
        nc.gpsimd.tensor_scalar(out=sgn[:], in0=sgn[:], scalar1=-1.0, scalar2=None, op0=ALU.add)
        nc.gpsimd.tensor_tensor(out=gabs[:], in0=g_raw[:], in1=sgn[:], op=ALU.mult)
        nc.gpsimd.tensor_tensor(out=gb[:], in0=b_raw[:], in1=gabs[:], op=ALU.mult)

        wm_w = keep.tile([P, 2, 4, 2 * P], U8, name="wm_w", align_bytes=64)
        wm_sc = keep.tile([P, 2, 4, P], U8, name="wm_sc", align_bytes=64)

        def permute_wm(z, a):
            nc.vector.tensor_copy(
                out=wm_w[:, a].rearrange("p t (m b) -> p t m b", b=2),
                in_=wm_raw[:].rearrange("p (a m t b) -> p a t m b", a=2, t=4, b=2)[:, a],
            )
            nc.vector.tensor_copy(out=wm_sc[:, a], in_=wm_sc_raw[:].rearrange("p (a m t) -> p a t m", a=2, t=4)[:, a])

        m_bf, mbank, mgrp, mq, mqs = {}, {}, {}, {}, {}

        def widen(c, j):
            n = 1 if c == 0 else 2
            if n * j % 2 == 0:
                m_bf[c, n * j // 2] = mpool.tile([P, 2, S], BF16, tag="m_bf", name="m_bf_t", bufs=6)
            t = m_bf[c, n * j // 2]
            o = n * j % 2
            nc.vector.tensor_tensor(
                out=t[:, o : o + n, :].rearrange("p i k -> p (i k)"),
                in0=m_u8[c][:, n * j : n * j + n, :].rearrange("p i k -> p (i k)").bitcast(F8),
                in1=scale_bc[:, 0:n, :].rearrange("p i k -> p (i k)"),
                op=ALU.mult,
            )

        def turn_pe(c, h):
            mbank[c, h] = ps_s.tile([P, 2, 2, P], F32, tag="s", name="mbank_t")
            for j in range(2):
                words = m_bf[c, h][:, j, :].bitcast(F32)
                for u in range(2):
                    nc.tensor.transpose(mbank[c, h][:, j, u, :], words[:, u : S // 2 : 2], ident_f[:])

        def turn_out(c, h):
            if c not in mgrp:
                mgrp[c] = mpool.tile([P, CHUNK, P, 4], BF16, tag="m_grouped", name="m_grouped", bufs=3, align_bytes=64)
            nc.scalar.copy(
                out=mgrp[c][:, 2 * h : 2 * h + 2].rearrange("p j r t -> p (j r t)").bitcast(F32).rearrange("p (j r u) -> p j r u", j=2, u=2),
                in_=mbank[c, h][:].rearrange("p j u r -> p j r u"),
            )

        def quant_m(c, z):
            mq[c] = qpool.tile([P, COLS], U32, tag="mq", name="mq_t", align_bytes=64)
            mqs[c] = qpool.tile([P, COLS], U8, tag="mqs", name="mqs_t", align_bytes=64)
            nc.vector.quantize_mx(out=mq[c][:].bitcast(E4M3), scales=mqs[c][:], in_=mgrp[c][:].rearrange("p j r t -> p (j r t)"))

        hbank, planes, grouped, aq, aqs = {}, {}, {}, {}, {}

        def embed_pe(k, t):
            c, a = divmod(k, 2)
            hbank[k, t] = ps_s.tile([P, COLS], F32, tag="s", name="hbank_t")
            nc.tensor.matmul_mx(
                out=hbank[k, t][:],
                lhsT=wm_w[:, a, t, :].bitcast(E2M1),
                lhsT_scale=wm_sc[:, a, t, :],
                rhs=mq[c][:].bitcast(E4M3),
                rhs_scale=mqs[c][:],
                start=True,
                stop=True,
            )

        def embed_out(k, t):
            a = k % 2
            if k not in planes:
                planes[k] = apool.tile([P, 4, COLS], BF16, tag="planes", name="planes_t")
            nc.scalar.activation(
                out=planes[k][:, t, :], in_=hbank[k, t][:], func=ACT.Relu, bias=gb[:, a, t : t + 1], scale=gabs[:, a, t : t + 1]
            )

        def apply_sign(k, t):
            a = k % 2
            nc.vector.tensor_scalar(
                out=planes[k][:, t, :], in0=planes[k][:, t, :], scalar1=sgn[:, a, t : t + 1], scalar2=None, op0=ALU.mult
            )

        def interleave(k, n0, n1, copy):
            if k not in grouped:
                grouped[k] = apool.tile([P, COLS, 4], BF16, tag="a_grouped", name="a_grouped", align_bytes=64)
            copy(
                out=grouped[k][:, n0:n1, :].rearrange("p (n i) t -> p n t i", i=4),
                in_=planes[k][:, :, n0:n1].rearrange("p t (n i) -> p n t i", i=4),
            )

        def interleave_v(k, z):
            interleave(k, S_SHARE.get(k, 0), COLS, nc.vector.tensor_copy)

        def interleave_s(k, z):
            interleave(k, 0, S_SHARE[k], nc.scalar.copy)

        def quant_a(k, z):
            aq[k] = qpool.tile([P, COLS], U32, tag="aq", name="aq_t", align_bytes=64, bufs=6)
            aqs[k] = qpool.tile([P, COLS], U8, tag="aqs", name="aqs_t", align_bytes=64, bufs=6)
            nc.vector.quantize_mx(out=aq[k][:].bitcast(E4M3), scales=aqs[k][:], in_=grouped[k][:].rearrange("p n t -> p (n t)"))

        sums, neg_mu, xt_ps, xc, rstd = {}, {}, {}, {}, {}

        def mean_pe(s, z):
            sums[s] = ps_s.tile([P, CB], F32, tag="s", name="sums_t")
            for cb in range(CB):
                for i in range(TILES):
                    nc.tensor.matmul(
                        out=sums[s][:, cb : cb + 1],
                        lhsT=x_sb[s][:, i, cb * P : (cb + 1) * P],
                        rhs=ones[:],
                        start=(i == 0),
                        stop=(i == TILES - 1),
                    )

        def mean_out(s, z):
            neg_mu[s] = xpool.tile([P, CB], F32, tag="neg_mu", name="neg_mu_t")
            nc.scalar.activation(out=neg_mu[s][:], in_=sums[s][:], func=ACT.Copy, scale=-1.0 / T)

        def center_pe(s, cb):
            xt_ps[s, cb] = ps_s.tile([P, TILES, P], BF16, tag="s", name="xt_ps_t")
            for i in range(TILES):
                nc.tensor.transpose(xt_ps[s, cb][:, i, :], x_sb[s][:, i, cb * P : (cb + 1) * P], ident_b[:])

        def center_out(s, cb):
            xc[s, cb] = xpool.tile([P, TILES, P], F32, tag="xc", name="xc_t")
            nc.scalar.activation(out=xc[s, cb][:], in_=xt_ps[s, cb][:], func=ACT.Identity, bias=neg_mu[s][:, cb : cb + 1])

        def variance(s, cb):
            junk = xpool.tile([P, TILES, P], BF16, tag="junk", name="junk", bufs=1)
            ss = xpool.tile([P, 1], F32, tag="ss", name="ss")
            nc.scalar.activation(out=junk[:], in_=xt_ps[s, cb][:], func=ACT.Square, bias=neg_mu[s][:, cb : cb + 1], accum_out=ss[:])
            rstd[s, cb] = xpool.tile([P, 1], F32, tag="rstd", name="rstd_t")
            nc.gpsimd.tensor_scalar(out=ss[:], in0=ss[:], scalar1=1.0 / T, scalar2=1e-5, op0=ALU.mult, op1=ALU.add)
            nc.gpsimd.tensor_tensor(out=rstd[s, cb][:], in0=ss[:], in1=minus_half[:], op=ALU.pow)

        gam, bet, t1s, ys, lks, obank = {}, {}, {}, {}, {}, {}

        def project(c, cb, w, banks):
            banks[c, cb] = ps_gb.tile([P, COLS], F32, tag="gb", name="banks_t")
            for a in range(2):
                nc.tensor.matmul_mx(
                    out=banks[c, cb][:],
                    lhsT=wgb[:, w + a, 2 * P * cb : 2 * P * (cb + 1)].bitcast(E2M1),
                    lhsT_scale=wgb_sc[:, w + a, P * cb : P * (cb + 1)],
                    rhs=aq[2 * c + a][:].bitcast(E4M3),
                    rhs_scale=aqs[2 * c + a][:],
                    start=(a == 0),
                    stop=(a == 1),
                )

        def modulate(c, cb):
            s, i0 = c // 2, (c % 2) * CHUNK
            t1s[c, cb] = ypool.tile([P, COLS], F32, tag="t1", name="t1_t")
            nc.vector.scalar_tensor_tensor(
                out=t1s[c, cb][:],
                in0=gam[c, cb][:],
                scalar=1.0,
                in1=xc[s, cb][:, i0 : i0 + CHUNK, :].rearrange("p i r -> p (i r)"),
                op0=ALU.add,
                op1=ALU.mult,
            )

        def shift(c, cb):
            ys[c, cb] = ypool.tile([P, COLS], F32, tag="y", name="y_t")
            nc.vector.scalar_tensor_tensor(
                out=ys[c, cb][:], in0=t1s[c, cb][:], scalar=rstd[c // 2, cb][:], in1=bet[c, cb][:], op0=ALU.mult, op1=ALU.add
            )

        def span(c, cb):
            return (cb, 0, CHUNK) if (c, cb) not in ((3, 3), (3, 4)) else (3, 2 * (cb - 3), 2 * (cb - 2))

        def leaky(c, b):
            cb, i0, i1 = span(c, b)
            y = ys[c, cb][:, i0 * P : i1 * P]
            lks[c, b] = ypool.tile([P, CHUNK, P], F32, tag="lk", name="lk_t")
            nc.vector.scalar_tensor_tensor(
                out=lks[c, b][:, 0 : i1 - i0, :].rearrange("p i r -> p (i r)"), in0=y, scalar=0.2, in1=y, op0=ALU.mult, op1=ALU.max
            )

        def out_pe(c, b):
            cb, i0, i1 = span(c, b)
            obank[c, b] = ps_s.tile([P, CHUNK, P], F32, tag="s", name="obank_t")
            for i in range(i1 - i0):
                nc.tensor.transpose(obank[c, b][:, i, :], lks[c, b][:, i, :], ident_f[:])

        def out_store(c, b):
            cb, i0, i1 = span(c, b)
            s, j0 = c // 2, (c % 2) * CHUNK
            res = ypool.tile([P, CHUNK, P], F32, tag="res", name="res_t")
            nc.scalar.copy(out=res[:, 0 : i1 - i0, :], in_=obank[c, b][:, 0 : i1 - i0, :])
            nc.sync.dma_start(
                out=out[s].rearrange("(p i) c -> p i c", i=TILES)[:, j0 + i0 : j0 + i1, cb * P : (cb + 1) * P],
                in_=res[:, 0 : i1 - i0, :],
            )

        calls = {
            "W": widen, "P": permute_wm, "T": turn_pe, "X": turn_out, "MQ": quant_m,
            "EP": embed_pe, "E": embed_out, "SG": apply_sign, "CP": interleave_v, "CS": interleave_s, "AQ": quant_a,
            "MP": mean_pe, "M": mean_out, "NP": center_pe, "N": center_out, "Q": variance,
            "GM": lambda c, b: project(c, b, 0, gam), "BT": lambda c, b: project(c, b, 2, bet),
            "V1": modulate, "V2": shift, "V3": leaky, "OP": out_pe, "O": out_store,
        }

        def needs(name, a, b):
            if name == "T":
                return [("W", a, 2 * b), ("W", a, 2 * b + 1)] if a == 0 else [("W", a, b)]
            if name == "X":
                return [("T", a, b)]
            if name == "MQ":
                return [("X", a, 0), ("X", a, 1)]
            if name == "EP":
                return [("MQ", a // 2, 0), ("P", 0, a % 2)]
            if name == "E":
                return [("EP", a, b)]
            if name == "SG":
                return [("E", a, b)]
            if name in ("CP", "CS"):
                return [("SG", a, t) for t in range(4)]
            if name == "AQ":
                return [("CP", a, 0)] + ([("CS", a, 0)] if a in S_SHARE else [])
            if name == "M":
                return [("MP", a, 0)]
            if name in ("N", "Q"):
                return [("M", a, 0), ("NP", a, b)]
            if name in ("GM", "BT"):
                return [("AQ", 2 * a, 0), ("AQ", 2 * a + 1, 0)]
            if name == "V1":
                return [("GM", a, b), ("N", a // 2, b)]
            if name == "V2":
                return [("V1", a, b), ("BT", a, b), ("Q", a // 2, b)]
            if name == "V3":
                return [("V2", a, span(a, b)[0])]
            if name == "OP":
                return [("V3", a, b)]
            if name == "O":
                return [("OP", a, b)]
            return []

        ctx.enter_context(tc.manual_schedule())
        queues = []
        for text in (VECTOR, SCALAR, TENSOR):
            words = [w.split(".") for w in text.split()]
            queues.append([(w[0], int(w[1]), int(w[2])) for w in words])
        written = set()
        while any(queues):
            for queue in queues:
                while queue and all(n in written for n in needs(*queue[0])):
                    call = queue.pop(0)
                    calls[call[0]](call[1], call[2])
                    written.add(call)
